import numpy as np, ml_dtypes
CORES = [83,85,87,115,117,119]
N = 6
import mx_ref
BF = ml_dtypes.bfloat16
def f(rng, *shape):
    return mx_ref.flush((rng.standard_normal(shape, dtype=np.float32) * np.exp2(rng.integers(-2, 3, shape[:-1] + (1,)))).astype(BF))
def wide(rng, *shape, cols=0):
    v = rng.standard_normal(shape, dtype=np.float32) * np.exp2(rng.integers(-12, 13, shape)).astype(np.float32)
    if cols: v *= np.repeat(np.exp2(rng.integers(-cols, cols + 1, shape[:-2] + (1, shape[-1] // 4))) * (rng.random(shape[:-2] + (1, shape[-1] // 4)) > 0.0625), 4, axis=-1).astype(np.float32)
    return mx_ref.flush(v.astype(BF))
def cols(t, e):
    v = np.concatenate([t.reshape(128, -1, 4), np.zeros((128, 1, 4), BF)], axis=1)
    return np.ascontiguousarray(v[:, e]).reshape(128, -1)
def tile(rs):
    return np.stack(rs, axis=2).reshape(128, -1).astype(BF)
def cut(t, i, w=512):
    return t[:, w * i:w * i + w]
def decode(q):
    o = []
    for b in range(4):
        e = np.zeros((128, 128, 4), np.float32); e[np.arange(128), np.arange(128), b] = 1
        o.append(mx_ref.matmul(mx_ref.quantize(e.reshape(128, 512).astype(BF)), q))
    return np.stack(o, axis=2).reshape(128, -1)
T, CK = 384, 96
def gates(g):
    t = np.zeros((128, 512), BF); t[:, :4 * N] = g
    return np.stack([t] * N)
def plus(g):
    return np.maximum(np.abs(g.astype(np.float32)), np.float32(0.0625)).astype(BF)
def apart(rng):
    g = np.zeros((128, 4 * N), BF)
    for e in range(N): g[8 * e:8 * e + 8, 4 * e:4 * e + 4] = plus(f(rng, 8, 4))
    return g
def setup_inputs(rng):
    return {"x": f(rng, N, 128, 4 * T), "wg": gates(f(rng, 128, 4 * N)), "w1": f(rng, N, 128, 2048)}
def setup_inputs_alike(rng):
    d = setup_inputs(rng); d["wg"] = gates(np.tile(f(rng, 128, 4), (1, N))); return d
def setup_inputs_ties(rng):
    d = setup_inputs(rng); d["wg"] = gates(plus(f(rng, 128, 4 * N))); d["x"] = -plus(d["x"])
    for s in range(N):
        k = rng.permutation(np.arange(T) // 5 if s % 2 else np.arange(T) % (T // (CK + 1)))
        d["x"][s] = d["x"][s].reshape(128, T, 4)[:, k].reshape(128, -1)
    return d
def setup_inputs_split(rng):
    d = setup_inputs(rng); g = apart(rng)
    v = d["x"].astype(np.float32).reshape(N, 128, T, 4)
    for s in range(N):
        p = rng.permutation(T)
        for e in range(N):
            sign = np.full((1, T, 1), -1, np.float32); sign[:, p[(e * CK + np.arange(CK)) % T]] = 1
            v[s, 8 * e:8 * e + 8] = np.abs(v[s, 8 * e:8 * e + 8]) * sign
    d["x"] = v.reshape(N, 128, 4 * T).astype(BF); d["wg"] = gates(g); return d
def setup_inputs_zeros(rng):
    d = setup_inputs(rng); g = apart(rng)
    v = d["x"].astype(np.float32).reshape(N, 128, T, 4)
    for s in range(N):
        for e in range(N):
            p = rng.permutation(T); u = np.abs(v[s, 8 * e:8 * e + 8])
            u[:, p[CK // 2:CK // 2 + CK]] = np.where(rng.random((8, CK, 4)) < 0.5, np.float32(-0.0), np.float32(0.0))
            u[:, p[CK // 2 + CK:]] *= np.float32(-1)
            v[s, 8 * e:8 * e + 8] = u
    d["x"] = v.reshape(N, 128, 4 * T).astype(BF); d["wg"] = gates(g); return d
def setup_inputs_spread(rng):
    d = setup_inputs(rng); d["x"] = wide(rng, N, 128, 4 * T, cols=6); return d
def check_inputs(d):
    b = []
    g = d["wg"].astype(np.float32)
    if (g != g[0]).any() or (g[:, :, 4 * N:] != 0).any(): b.append("wg")
    return b
def reference(x, wg, w1):
    took = []
    for s in range(N):
        z = mx_ref.matmul(mx_ref.quantize(wg[s]), mx_ref.quantize(x[s])) + np.float32(0.0)
        took.append([np.argsort(-z[e], kind="stable")[:CK] for e in range(N)])
    y = np.zeros((N, 128, T, 4), np.float32)
    for e in range(N):
        q = mx_ref.quantize(np.concatenate([cols(x[s], took[s][e]) for s in range(N)], axis=1))
        rs = [np.maximum(mx_ref.matmul(mx_ref.quantize(np.ascontiguousarray(cut(w1[e], i))), q), np.float32(0.0)) * np.float32(0.05) for i in range(4)]
        v = decode(mx_ref.quantize(tile(rs))).reshape(128, N, CK, 4)
        for s in range(N): y[s][:, took[s][e]] += v[:, s]
    return {"y": y.reshape(N, 128, 4 * T)}

@@ -1,0 +1,361 @@
+from concourse.bass import DstId, RemoteDMATransfer
+from concourse.mybir import dt, AluOpType, ActivationFunctionType
+
+OP = AluOpType
+AF = ActivationFunctionType
+NT, CK, N = 384, 96, 6
+BIG = 1e29
+F8, U8, F32, BF, U16, I32 = "float8_e4m3fn_x4", "uint8", "float32", "bfloat16", "uint16", "int32"
+
+FAR0, NEAR0, OWN0, ALLC = 0, 3 * CK, 5 * CK, 5 * CK + 128
+NCMP = NT // 16
+
+SHAPES = {
+    BF: {"xsb": 4 * NT, "wgs": 32, "wga": 512, "w1s": 2048, "ones": 512, "et": 2048, "reset16": 576, "reset4": 864,
+         "cmp": NCMP * NT, "eqw": NT, "corr": NT, "xt": 4 * ALLC, "rt": 4 * ALLC},
+    F8: {"qx": NT, "qg": 128, "qw": 512, "qe": 512, "ct": ALLC, "rxn": 192, "rxf": 288, "rc": ALLC, "bkn": 192, "bkf": 288},
+    U8: {"px": NT, "pg": 128, "pw": 512, "pe": 512, "cs": ALLC, "rxns": 192, "rxfs": 288, "rs": ALLC, "bkns": 192, "bkfs": 288},
+    I32: {"pi": 2, "p3i": 2, "p15i": 2, "pmi": 2},
+    U16: {"offw": 32, "offr": NCMP, "off4": 144, "off16": 36, "offc": 216},
+    F32: {"p3": 2, "p15": 2, "pm": 2, "offwf": 32, "k16": 576, "k4": 864, "tok": NT, "slots": 576, "m3": NT, "rr": NT,
+          "mask4": CK, "mcol": 4, "mcol16": 16, "md": NT, "sc": NT, "acc": NCMP, "rk": NCMP, "win": NT, "t1": 128, "t2": 96,
+          "bl": 576, "sel1": 576, "sel2": 576, "s16": 576, "s16b": 576, "cl": 864, "cm": 864, "cq": 864,
+          "dd": 8 + 4 * 576, "aa": 8 + 4 * 576, "yy": 4 * NT},
+}
+SCRATCH = {name: ("sbuf", [128, n], kind) for kind in SHAPES for name, n in SHAPES[kind].items()}
+SCRATCH["pp"] = ("psum", [128, 4096], F32)
+SEMAPHORES = ["sv", "sa", "sten", "sp", "ldx", "ldg", "ldw", "sty", "sty2", "loc", "dn", "df", "rn", "rf"]
+
+
+def rank_program(g, core, T, topo):
+    me = T.rank_of(core)
+    if me is None:
+        return
+    cores = list(T.cores)
+
+    def far_of(r):
+        return [k for k in range(N) if topo.chip(cores[k]) != topo.chip(cores[r])]
+
+    def near_of(r):
+        return [k for k in range(N) if k != r and topo.chip(cores[k]) == topo.chip(cores[r])]
+
+    far, near = far_of(me), near_of(me)
+    order = far + near + [me]
+    group_of = {e: (0, 2, 4, 6, 1, 3)[i] for i, e in enumerate(order)}
+    expert_of = [far[0]] * 8
+    for e in order:
+        expert_of[group_of[e]] = e
+    pos = {e: CK * i for i, e in enumerate(order)}
+
+    Q = {"v": (g.vector, "sv"), "a": (g.scalar, "sa"), "t": (g.tensor, "sten"), "p": (g, "sp"), "s": (g.sync, None)}
+    count = {"sv": 0, "sa": 0, "sten": 0, "sp": 0}
+    seen = {}
+
+    def need(q, deps):
+        for d in deps:
+            if d is not None and seen.get((q, d[0]), 0) < d[1]:
+                Q[q][0].wait_ge(T.sem[d[0]], d[1])
+                seen[(q, d[0])] = d[1]
+
+    def done(q, ins):
+        s = Q[q][1]
+        ins.then_inc(T.sem[s], 1)
+        count[s] += 1
+        if q == "p":
+            need("p", [(s, count[s])])
+        return (s, count[s])
+
+    V, A, TE = g.vector, g.scalar, g.tensor
+
+    g.sync.dma_start(T.xsb[:], T.x[:]).then_inc(T.sem["ldx"], 16)
+    g.scalar.dma_start(T.wgs[:], T.wg[:, 0:32]).then_inc(T.sem["ldg"], 16)
+    g.sync.dma_start(T.w1s[:], T.w1[:]).then_inc(T.sem["ldw"], 16)
+    LDX, LDG, LDW = ("ldx", 16), ("ldg", 16), ("ldw", 16)
+
+    def iota(name, pattern, base, cm):
+        if name == "pi":
+            return done("p", g.iota(T.pi[:], pattern, base, cm))
+        return done("p", g.iota(T[name][:], pattern, base, cm, allow_small_or_imprecise_dtypes=True))
+
+    c_pi = iota("pi", [[0, 2]], 0, 1)
+    c_k16 = iota("k16", [[0, 36], [1, 16]], 0, 0)
+    c_k4 = iota("k4", [[0, 216], [1, 4]], 0, 0)
+    c_tok = iota("tok", [[1, NT]], 0, 0)
+    c_slots = iota("slots", [[1, 576]], 1, 0)
+
+    for k in range(8):
+        c_off = done("v", V.memset(T.offwf[:, 4 * k:4 * k + 4], float(4 * expert_of[k])))
+    need("v", [c_pi])
+    c_p3i = done("v", V.tensor_scalar(T.p3i[:], T.pi[:], 3, None, OP.bitwise_and))
+    c_p15i = done("v", V.tensor_scalar(T.p15i[:], T.pi[:], 15, None, OP.bitwise_and))
+    c_pmi = done("v", V.tensor_scalar(T.pmi[:], T.pi[:], 15, 2, OP.bitwise_and, OP.logical_shift_right))
+    need("v", [c_p3i])
+    c_p3 = done("v", V.tensor_copy(T.p3[:], T.p3i[:]))
+    need("v", [c_p15i, c_pmi])
+    c_p15 = done("v", V.tensor_copy(T.p15[:], T.p15i[:]))
+    c_pm = done("v", V.tensor_copy(T.pm[:], T.pmi[:]))
+    need("v", [c_off, c_p3])
+    c_offw = done("v", V.tensor_scalar(T.offw[:], T.offwf[:], T.p3[:, 0:1], None, OP.add))
+    need("v", [c_k16, c_pm])
+    c_m3 = done("v", V.tensor_scalar(T.m3[:], T.k16[:, 0:NT], T.p15[:, 0:1], -BIG, OP.not_equal, OP.mult))
+    c_ones = done("v", V.memset(T.ones[:], 1.0))
+
+    need("a", [c_k16])
+    c_r16 = done("a", A.activation(T.reset16[:], T.k16[:], AF.Sign))
+    need("a", [c_offw, LDG])
+    a_wga = done("a", A.activation(T.wga[:], T.wgs[:, 0:32].indirect(T.offw[:, 0:32]), AF.Copy))
+    need("a", [c_r16])
+    c_rr = done("a", A.activation(T.rr[:], T.reset16[:, 0:NT], AF.Copy, bias=-BIG, scale=BIG))
+    need("a", [c_k4])
+    c_r4 = done("a", A.activation(T.reset4[:], T.k4[:], AF.Sign))
+
+    need("p", [c_ones])
+    for b in range(4):
+        c_et = done("p", g.affine_select(T.et[:, 512 * b:512 * b + 512], T.ones[:], [[-1, 512]], OP.is_equal, 0.0, b, 4))
+
+    need("v", [a_wga])
+    v_qg = done("v", V.quantize_mx(T.qg[:], T.pg[:], T.wga[:]))
+    need("v", [LDX])
+    v_qx = done("v", V.quantize_mx(T.qx[:], T.px[:], T.xsb[:]))
+    need("t", [v_qg, v_qx])
+    Z = T.pp[:, 0:NT]
+    t_z = done("t", TE.matmul_mx(Z, T.qg[:], T.pg[:], T.qx[:], T.px[:], True, True))
+    need("v", [c_k4])
+    c_m4 = done("v", V.tensor_scalar(T.mask4[:], T.k4[:, 0:CK], T.pm[:, 0:1], 4.0, OP.is_equal, OP.mult))
+
+    need("v", [t_z, c_m3])
+    v_md = done("v", V.tensor_tensor(T.md[:], Z, T.m3[:], OP.add))
+    need("v", [v_md, c_rr])
+    v_sc = done("v", V.tensor_tensor_scan(T.sc[:], T.rr[:], T.md[:], 0.0, OP.add, OP.max))
+    need("v", [v_sc])
+    for q in range(NCMP):
+        s = T.sc[:, 16 * q + 15:16 * q + 16]
+        cut = 16 * q + 16
+        v_c = done("v", V.tensor_scalar(T.cmp[:, NT * q:NT * q + cut], T.pp[:, 0:cut], s, None, OP.is_ge))
+        if cut < NT:
+            v_c = done("v", V.tensor_scalar(T.cmp[:, NT * q + cut:NT * q + NT], T.pp[:, cut:NT], s, None, OP.is_gt))
+        need("a", [v_c])
+        row = T.cmp[:, NT * q:NT * q + NT]
+        a_acc = done("a", A.activation(row, row, AF.Copy, accum_out=T.acc[:, q:q + 1]))
+    v_eq = done("v", V.tensor_tensor(T.eqw[:], Z, T.sc[:], OP.is_equal))
+    need("v", [v_eq, c_r16])
+    v_corr = done("v", V.tensor_tensor_scan(T.corr[:], T.reset16[:, 0:NT], T.eqw[:], 0.0, OP.mult, OP.add))
+    need("v", [a_acc, v_corr])
+    v_rk = done("v", V.tensor_tensor(T.rk[:], T.acc[:], T.corr[:, 15:NT:16], OP.subtract))
+    need("v", [v_rk])
+    v_offr = done("v", V.tensor_copy(T.offr[:], T.rk[:]))
+    need("v", [v_offr, c_tok])
+    v_win = done("v", V.tensor_copy(T.win[:, 0:NT].indirect(T.offr[:, 0:NCMP]), T.tok[:]))
+
+    c_t1 = done("v", V.memset(T.t1[:, 96:128], 0.0))
+    need("v", [v_win])
+    v_t1 = done("v", V.transpose(T.t1[:, 0:96], T.win[:, 0:96]))
+    need("v", [v_t1])
+    v_t2 = done("v", V.transpose(T.t2[:, 0:96], T.t1[:, 16:112]))
+    bc = {}
+    for e in order:
+        k = group_of[e]
+        p0 = 32 * (k // 2)
+        need("p", [v_win if k % 2 == 0 else v_t2])
+        bc[e] = done("p", g.partition_broadcast(T.bl[:, CK * e:CK * e + CK], T["win" if k % 2 == 0 else "t2"][p0:p0 + 1, 0:CK], 128))
+
+    off = {}
+
+    def offsets(e):
+        c = slice(CK * e, CK * e + CK)
+        need("v", [bc[e], c_m4])
+        d = done("v", V.tensor_tensor(T.sel1[:, c], T.bl[:, c], T.mask4[:], OP.mult))
+        need("v", [d, c_r4])
+        d = done("v", V.tensor_tensor_scan(T.sel2[:, c], T.reset4[:, 0:CK], T.sel1[:, c], 0.0, OP.mult, OP.add))
+        need("v", [d])
+        off[e] = done("v", V.tensor_scalar(T.off4[:, 24 * e:24 * e + 24], T.sel2[:, CK * e + 3:CK * e + CK:4], T.p3[:, 0:1], None, OP.add))
+
+    def gather(q, e):
+        out = T.xt[:, 4 * pos[e]:4 * pos[e] + 4 * CK]
+        win = T.xsb[:, 0:4 * NT].indirect(T.off4[:, 24 * e:24 * e + 24])
+        need(q, [off[e]])
+        return done(q, A.activation(out, win, AF.Copy) if q == "a" else V.tensor_copy(out, win))
+
+    def pack(lo, hi, deps, src, qc, qs):
+        need("v", deps)
+        return done("v", V.quantize_mx(T[qc][:, lo:hi], T[qs][:, lo:hi], T[src][:, 4 * lo:4 * hi]))
+
+    for e in far:
+        offsets(e)
+    a_gf = [gather("a", e) for e in far[:2]][-1]
+    v_gf = gather("v", far[2])
+    v_qfar = pack(FAR0, NEAR0, [a_gf, v_gf], "xt", "ct", "cs")
+    offsets(near[0])
+    a_gn = gather("a", near[0])
+    offsets(near[1])
+    v_gn = gather("v", near[1])
+    v_qnear = pack(NEAR0, OWN0, [a_gn, v_gn], "xt", "ct", "cs")
+    offsets(me)
+    a_go = gather("a", me)
+    c_xpad = done("v", V.memset(T.xt[:, 4 * (OWN0 + CK):4 * ALLC], 0.0))
+
+    local = [0]
+
+    def lanes(isfar, bits, i):
+        if not isfar:
+            return (8 + 4 * i, 12 + 4 * i)
+        return (2 * i, 2 * i + 2) if bits else ((6, 7), (7, 8), (0, 4))[i]
+
+    def arrivals(isfar):
+        n = 0
+        for r in (far if isfar else near):
+            i = (far_of(r) if isfar else near_of(r)).index(me)
+            for bits in (True, False):
+                lo, hi = lanes(isfar, bits, i)
+                n += hi - lo
+        return n
+
+    def send(isfar, dep, codes, planes, dcodes, dplanes, rsem):
+        need("p", [dep])
+        for bits, sname, dname in ((True, codes, dcodes), (False, planes, dplanes)):
+            tr = []
+            for i, r in enumerate(far if isfar else near):
+                lo, hi = lanes(isfar, bits, i)
+                es = topo.engines(core, cores[r])[lo:hi]
+                there = (far_of(r) if isfar else near_of(r)).index(me) * CK
+                src = T[sname][:, pos[r]:pos[r] + CK]
+                dst = T[dname][:, there:there + CK]
+                if bits:
+                    src, dst = src.bitcast(dt.uint8), dst.bitcast(dt.uint8)
+                ad = topo.addr(cores[r])
+                tr.append(RemoteDMATransfer(dst_ids=[DstId(rid=ad[0], pnc=ad[1])], dma_engine_mask=sum(1 << k for k in es), remote_sem=T.sem[rsem], src=src, dst=dst))
+                local[0] += len(es)
+            g.remote_dma_fused(tr, local_sem=T.sem["loc"])
+
+    send(True, v_qfar, "ct", "cs", "rxf", "rxfs", "df")
+    send(False, v_qnear, "ct", "cs", "rxn", "rxns", "dn")
+    DF, DN, RF, RN = ("df", arrivals(True)), ("dn", arrivals(False)), ("rf", arrivals(True)), ("rn", arrivals(False))
+
+    need("v", [LDW])
+    for i in range(4):
+        v_qw = done("v", V.quantize_mx(T.qw[:, 128 * i:128 * i + 128], T.pw[:, 128 * i:128 * i + 128], T.w1s[:, 512 * i:512 * i + 512]))
+    v_qown = pack(OWN0, ALLC, [a_go, c_xpad], "xt", "ct", "cs")
+
+    def products(stat, plane, codes, planes, lo, hi, bank, deps):
+        need("t", deps)
+        r = []
+        for i in range(4):
+            c = slice(128 * i, 128 * i + 128)
+            o = 512 * (bank + i)
+            r.append(done("t", TE.matmul_mx(T.pp[:, o:o + hi - lo], T[stat][:, c], T[plane][:, c], T[codes][:, lo:hi], T[planes][:, lo:hi], True, True)))
+        return r
+
+    def relu(q, lo, hi, bank, i, dep):
+        need(q, [dep])
+        o = 512 * (bank + i)
+        out, src = T.rt[:, 4 * lo + i:4 * hi:4], T.pp[:, o:o + hi - lo]
+        if q == "v":
+            return done("v", V.tensor_scalar(out, src, 0.0, 0.05, OP.max, OP.mult))
+        return done("a", A.activation(out, src, AF.Relu, scale=0.05))
+
+    def slot(e):
+        return 4 * (1 + CK * e)
+
+    def unpack(q, e0, n, bank, col, b, dep):
+        need(q, [dep])
+        o = 512 * (bank + b) + col
+        t = T.aa if e0 == 0 and n == CK else T.dd
+        out, src = t[:, slot(e0) + b:slot(e0) + 4 * n:4], T.pp[:, o:o + n]
+        return done(q, V.tensor_copy(out, src) if q == "v" else A.activation(out, src, AF.Copy))
+
+    need("v", [c_k4])
+    c_m16 = done("v", V.tensor_scalar(T.mcol16[:], T.k16[:, 0:16], T.p15[:, 0:1], None, OP.is_equal))
+    c_mcol = done("v", V.tensor_scalar(T.mcol[:], T.k4[:, 0:4], T.pm[:, 0:1], 4.0, OP.is_equal, OP.mult))
+    need("a", [c_m16, bc[order[-1]]])
+    for m in range(16):
+        a_s16 = done("a", A.activation(T.s16[:, m:576:16], T.bl[:, m:576:16], AF.Copy, scale=T.mcol16[:, m:m + 1]))
+
+    p_own = products("qw", "pw", "ct", "cs", OWN0, ALLC, 0, [v_qw, v_qown, v_eq])
+    r1 = [relu("v", OWN0, ALLC, 0, i, p_own[i]) for i in (0, 1)]
+    r2 = [relu("a", OWN0, ALLC, 0, i, p_own[i]) for i in (2, 3)]
+    v_rown = pack(OWN0, ALLC, [r1[-1], r2[-1]], "rt", "rc", "rs")
+    need("v", [c_et])
+    for i in range(4):
+        v_qe = done("v", V.quantize_mx(T.qe[:, 128 * i:128 * i + 128], T.pe[:, 128 * i:128 * i + 128], T.et[:, 512 * i:512 * i + 512]))
+    c_cl = done("v", V.memset(T.cl[:, 0:NT], 0.0))
+    c_aa = done("v", V.memset(T.aa[:, 0:4], 0.0))
+    need("v", [a_s16])
+    d = done("v", V.tensor_tensor_scan(T.s16b[:], T.reset16[:], T.s16[:], 0.0, OP.mult, OP.add))
+    need("v", [d])
+    v_o16 = done("v", V.tensor_copy(T.off16[:], T.s16b[:, 15:576:16]))
+
+    p_far = products("qw", "pw", "rxf", "rxfs", 0, 288, 4, [DF])
+    f1 = [relu("v", FAR0, NEAR0, 4, i, p_far[i]) for i in (0, 1)]
+    f2 = [relu("a", FAR0, NEAR0, 4, i, p_far[i]) for i in (2, 3)]
+    v_rfar = pack(FAR0, NEAR0, [f1[-1], f2[-1]], "rt", "rc", "rs")
+    send(True, v_rfar, "rc", "rs", "bkf", "bkfs", "rf")
+
+    p_near = products("qw", "pw", "rxn", "rxns", 0, 192, 0, [DN, r1[-1], r2[-1]])
+    e_near = [relu("a", NEAR0, OWN0, 0, i, p_near[i]) for i in range(4)]
+    v_rnear = pack(NEAR0, OWN0, [e_near[-1]], "rt", "rc", "rs")
+    send(False, v_rnear, "rc", "rs", "bkn", "bkns", "rn")
+
+    u_own = products("qe", "pe", "rc", "rs", OWN0, ALLC, 4, [v_rown, v_qe, f1[-1], f2[-1]])
+    d_own = [unpack("a", me, CK, 4, 0, b, u_own[b]) for b in range(4)]
+
+    last = None
+    need("v", [v_o16, c_cl, c_slots])
+    for e in range(N):
+        o16 = T.off16[:, 6 * e:6 * e + 6]
+        need("v", [last])
+        if e:
+            last = done("v", V.tensor_copy(T.cl[:, NT + CK * (e - 1):NT + CK * e], T.cl[:, 0:NT].indirect(o16)))
+            need("v", [last])
+        last = done("v", V.tensor_copy(T.cl[:, 0:NT].indirect(o16), T.slots[:, CK * e:CK * e + CK]))
+    need("a", [last, c_mcol])
+    for m in range(4):
+        a_cm = done("a", A.activation(T.cm[:, m:864:4], T.cl[:, m:864:4], AF.Copy, scale=T.mcol[:, m:m + 1]))
+    need("v", [a_cm, c_r4])
+    d = done("v", V.tensor_tensor_scan(T.cq[:], T.reset4[:], T.cm[:], 0.0, OP.mult, OP.add))
+    need("v", [d])
+    v_offc = done("v", V.tensor_scalar(T.offc[:], T.cq[:, 3:864:4], T.p3[:, 0:1], None, OP.add))
+
+    u_near = products("qe", "pe", "bkn", "bkns", 0, 192, 0, [RN, e_near[-1]])
+    d_near = [unpack("a", near[i], CK, 0, CK * i, b, u_near[b]) for b in range(4) for i in range(2)]
+    u_far = products("qe", "pe", "bkf", "bkfs", 0, 288, 4, [RF, d_own[-1]])
+
+    def chain(e, deps):
+        need("v", deps + [v_offc, c_aa])
+        o = 96 + 24 * (e - 1)
+        s = slice(slot(e), slot(e) + 4 * CK)
+        return done("v", V.tensor_tensor(T.aa[:, s], T.aa[:, 0:slot(e)].indirect(T.offc[:, o:o + 24]), T.dd[:, s], OP.add))
+
+    def far_unpack(q, b):
+        if far[0] == 0:
+            unpack(q, 0, CK, 4, 0, b, u_far[b])
+            return unpack(q, 1, 2 * CK, 4, CK, b, u_far[b])
+        return unpack(q, far[0], 3 * CK, 4, 0, b, u_far[b])
+
+    dlast = [d_own[-1], d_near[-1]]
+    step = None
+    if far[0] != 0:
+        for e in (1, 2):
+            step = chain(e, dlast + [step])
+    d1 = [far_unpack("v", b) for b in (0, 1)][-1]
+    d2 = [far_unpack("a", b) for b in (2, 3)][-1]
+    for e in range(1 if far[0] == 0 else 3, N):
+        step = chain(e, dlast + [d1, d2, step])
+
+    H = NT
+    win = T.aa[:, 0:slot(N)]
+    for q, quarters in (("v", (0, 1)), ("a", (2, 3))):
+        need(q, [step, v_offc])
+        r = []
+        for k in quarters:
+            out, src = T.yy[:, H * k:H * k + H], win.indirect(T.offc[:, 24 * k:24 * k + 24])
+            r.append(done(q, V.tensor_copy(out, src) if q == "v" else A.activation(out, src, AF.Copy)))
+        dq, sem = ("s", "sty") if q == "v" else ("a", "sty2")
+        for k, d in zip(quarters, r):
+            need(dq, [d])
+            Q[dq][0].dma_start(T.y[:, H * k:H * k + H], T.yy[:, H * k:H * k + H]).then_inc(T.sem[sem], 16)
+
+    g.wait_ge(T.sem["loc"], local[0])
+    for s in count:
+        g.wait_ge(T.sem[s], count[s])
+    g.wait_ge(T.sem["sty"], 32)
+    g.wait_ge(T.sem["sty2"], 32)

@@ -9,22 +9,26 @@ F8, U8, F32, BF, U16, I32 = "float8_e4m3fn_x4", "uint8", "float32", "bfloat16", 
 
 FAR0, NEAR0, OWN0, ALLC = 0, 3 * CK, 5 * CK, 5 * CK + 128
 NCMP = NT // 16
+NS = 9
+S0 = 16 * NS
+HALF = NT // 2
+NP = CK * (N - 1)
 
 SHAPES = {
     BF: {"xsb": 4 * NT, "wgs": 32, "wga": 512, "w1s": 2048, "ones": 512, "et": 2048, "reset16": 576, "reset4": 864,
-         "cmp": NCMP * NT, "eqw": NT, "corr": NT, "xt": 4 * ALLC, "rt": 4 * ALLC},
+         "cmp": NCMP * NT, "sums": (NCMP - NS) * HALF, "eqw": NT, "corr": NT, "xt": 4 * ALLC, "rt": 4 * ALLC},
     F8: {"qx": NT, "qg": 128, "qw": 512, "qe": 512, "ct": ALLC, "rxn": 192, "rxf": 288, "rc": ALLC, "bkn": 192, "bkf": 288},
     U8: {"px": NT, "pg": 128, "pw": 512, "pe": 512, "cs": ALLC, "rxns": 192, "rxfs": 288, "rs": ALLC, "bkns": 192, "bkfs": 288},
     I32: {"pi": 2, "p3i": 2, "p15i": 2, "pmi": 2},
     U16: {"offw": 32, "offr": NCMP, "off4": 144, "off16": 36, "offc": 216},
     F32: {"p3": 2, "p15": 2, "pm": 2, "offwf": 32, "k16": 576, "k4": 864, "tok": NT, "slots": 576, "m3": NT, "rr": NT,
-          "mask4": CK, "mcol": 4, "mcol16": 16, "md": NT, "sc": NT, "acc": NCMP, "rk": NCMP, "win": NT, "t1": 128, "t2": 96,
-          "bl": 576, "sel1": 576, "sel2": 576, "s16": 576, "s16b": 576, "cl": 864, "cm": 864, "cq": 864,
-          "dd": 8 + 4 * 576, "aa": 8 + 4 * 576, "yy": 4 * NT},
+          "mask4": CK, "mcol": 4, "mcol16": 16, "md": NT, "sc": NT, "acc": NS, "acc2": NS, "acc3": NS, "rk": NS, "rk2": NS,
+          "first": NCMP, "win": NT, "t1": 128, "t2": 96, "bl": 576, "sel1": 576, "sel2": 576, "s16": 576, "s16b": 576,
+          "cl": NP + NT, "cm": NP + NT, "cq": NP + NT, "dd": 8 + 4 * 576, "aa": 8 + 4 * 576, "yy": 4 * NT},
 }
 SCRATCH = {name: ("sbuf", [128, n], kind) for kind in SHAPES for name, n in SHAPES[kind].items()}
 SCRATCH["pp"] = ("psum", [128, 4096], F32)
-SEMAPHORES = ["sv", "sa", "sten", "sp", "ldx", "ldg", "ldw", "sty", "sty2", "loc", "dn", "df", "rn", "rf"]
+SEMAPHORES = ["sv", "sa", "sten", "sp", "ldx", "ldx2", "ldg", "ldw", "sty", "sty2", "loc", "dn", "df", "rn", "rf"]
 
 
 def rank_program(g, core, T, topo):
@@ -67,10 +71,11 @@ def rank_program(g, core, T, topo):
 
     V, A, TE = g.vector, g.scalar, g.tensor
 
-    g.sync.dma_start(T.xsb[:], T.x[:]).then_inc(T.sem["ldx"], 16)
+    g.sync.dma_start(T.xsb[:, 0:4 * HALF], T.x[:, 0:4 * HALF]).then_inc(T.sem["ldx"], 16)
     g.scalar.dma_start(T.wgs[:], T.wg[:, 0:32]).then_inc(T.sem["ldg"], 16)
+    g.sync.dma_start(T.xsb[:, 4 * HALF:4 * NT], T.x[:, 4 * HALF:4 * NT]).then_inc(T.sem["ldx2"], 16)
     g.sync.dma_start(T.w1s[:], T.w1[:]).then_inc(T.sem["ldw"], 16)
-    LDX, LDG, LDW = ("ldx", 16), ("ldg", 16), ("ldw", 16)
+    LDX, LDX2, LDG, LDW = ("ldx", 16), ("ldx2", 16), ("ldg", 16), ("ldw", 16)
 
     def iota(name, pattern, base, cm):
         if name == "pi":
@@ -99,6 +104,10 @@ def rank_program(g, core, T, topo):
     need("v", [c_k16, c_pm])
     c_m3 = done("v", V.tensor_scalar(T.m3[:], T.k16[:, 0:NT], T.p15[:, 0:1], -BIG, OP.not_equal, OP.mult))
     c_ones = done("v", V.memset(T.ones[:], 1.0))
+    c_t1 = done("v", V.memset(T.t1[:, 96:128], 0.0))
+    c_xpad = done("v", V.memset(T.xt[:, 4 * (OWN0 + CK):4 * ALLC], 0.0))
+    c_cl = done("v", V.memset(T.cl[:, NP:NP + NT], 0.0))
+    c_aa = done("v", V.memset(T.aa[:, 0:4], 0.0))
 
     need("a", [c_k16])
     c_r16 = done("a", A.activation(T.reset16[:], T.k16[:], AF.Sign))
@@ -116,83 +125,115 @@ def rank_program(g, core, T, topo):
     need("v", [a_wga])
     v_qg = done("v", V.quantize_mx(T.qg[:], T.pg[:], T.wga[:]))
     need("v", [LDX])
-    v_qx = done("v", V.quantize_mx(T.qx[:], T.px[:], T.xsb[:]))
+    done("v", V.quantize_mx(T.qx[:, 0:HALF], T.px[:, 0:HALF], T.xsb[:, 0:4 * HALF]))
+    need("v", [LDX2])
+    v_qx = done("v", V.quantize_mx(T.qx[:, HALF:NT], T.px[:, HALF:NT], T.xsb[:, 4 * HALF:4 * NT]))
     need("t", [v_qg, v_qx])
-    Z = T.pp[:, 0:NT]
-    t_z = done("t", TE.matmul_mx(Z, T.qg[:], T.pg[:], T.qx[:], T.px[:], True, True))
+    t_z, t_z2 = [done("t", TE.matmul_mx(T.pp[:, 512 * k:512 * k + NT], T.qg[:], T.pg[:], T.qx[:], T.px[:], True, True)) for k in (0, 1)]
+    Z, Z2 = T.pp[:, 0:NT], T.pp[:, 512:512 + NT]
     need("v", [c_k4])
     c_m4 = done("v", V.tensor_scalar(T.mask4[:], T.k4[:, 0:CK], T.pm[:, 0:1], 4.0, OP.is_equal, OP.mult))
+    c_m16 = done("v", V.tensor_scalar(T.mcol16[:], T.k16[:, 0:16], T.p15[:, 0:1], None, OP.is_equal))
+    c_mcol = done("v", V.tensor_scalar(T.mcol[:], T.k4[:, 0:4], T.pm[:, 0:1], 4.0, OP.is_equal, OP.mult))
 
+    parts = ((0, S0), (S0, NT))
     need("v", [t_z, c_m3])
-    v_md = done("v", V.tensor_tensor(T.md[:], Z, T.m3[:], OP.add))
-    need("v", [v_md, c_rr])
-    v_sc = done("v", V.tensor_tensor_scan(T.sc[:], T.rr[:], T.md[:], 0.0, OP.add, OP.max))
-    need("v", [v_sc])
-    for q in range(NCMP):
-        s = T.sc[:, 16 * q + 15:16 * q + 16]
-        cut = 16 * q + 16
-        v_c = done("v", V.tensor_scalar(T.cmp[:, NT * q:NT * q + cut], T.pp[:, 0:cut], s, None, OP.is_ge))
-        if cut < NT:
-            v_c = done("v", V.tensor_scalar(T.cmp[:, NT * q + cut:NT * q + NT], T.pp[:, cut:NT], s, None, OP.is_gt))
-        need("a", [v_c])
-        row = T.cmp[:, NT * q:NT * q + NT]
-        a_acc = done("a", A.activation(row, row, AF.Copy, accum_out=T.acc[:, q:q + 1]))
+    v_md = [done("v", V.tensor_tensor(T.md[:, lo:hi], T.pp[:, lo:hi], T.m3[:, lo:hi], OP.add)) for lo, hi in parts]
+    v_sc = []
+    for (lo, hi), d in zip(parts, v_md):
+        need("v", [d, c_rr])
+        v_sc.append(done("v", V.tensor_tensor_scan(T.sc[:, lo:hi], T.rr[:, lo:hi], T.md[:, lo:hi], 0.0, OP.add, OP.max)))
+
+    need("a", [t_z2, v_sc[0]])
+    signs = []
+    for q in range(NS + 1):
+        if q < NS:
+            signs.append(done("a", A.activation(T.cmp[:, NT * q:NT * q + NT], Z2, AF.Sign, bias=T.sc[:, 16 * q + 15:16 * q + 16], scale=-1.0)))
+        if q:
+            k, c = q - 1, NT * (q - 1)
+            lower, higher = T.cmp[:, c:c + 16 * q], T.cmp[:, c + 16 * q:c + NT]
+            need("a", [signs[k]])
+            done("a", A.activation(lower, lower, AF.Relu, accum_out=T.acc[:, k:k + 1]))
+            a_acc = done("a", A.activation(higher, higher, AF.Relu, scale=-1.0, accum_out=T.acc2[:, k:k + 1]))
+
+    def total(q, deps):
+        o, c = HALF * (q - NS), NT * q
+        need("v", deps)
+        return done("v", V.tensor_tensor_scan(T.sums[:, o:o + HALF], T.cmp[:, c:c + HALF], T.cmp[:, c + HALF:c + NT], T.first[:, q:q + 1], OP.add, OP.add))
+
+    need("v", [v_sc[1]])
     v_eq = done("v", V.tensor_tensor(T.eqw[:], Z, T.sc[:], OP.is_equal))
-    need("v", [v_eq, c_r16])
-    v_corr = done("v", V.tensor_tensor_scan(T.corr[:], T.reset16[:, 0:NT], T.eqw[:], 0.0, OP.mult, OP.add))
-    need("v", [a_acc, v_corr])
-    v_rk = done("v", V.tensor_tensor(T.rk[:], T.acc[:], T.corr[:, 15:NT:16], OP.subtract))
-    need("v", [v_rk])
-    v_offr = done("v", V.tensor_copy(T.offr[:], T.rk[:]))
+    late = []
+    for q in range(NS, NCMP):
+        s = T.sc[:, 16 * q + 15:16 * q + 16]
+        cut, c = 16 * q + 16, NT * q
+        d = done("v", V.tensor_scalar(T.cmp[:, c:c + cut], T.pp[:, 0:cut], s, None, OP.is_ge))
+        if cut < NT:
+            d = done("v", V.tensor_scalar(T.cmp[:, c + cut:c + NT], T.pp[:, cut:NT], s, None, OP.is_gt))
+        late.append((q, d))
+        if q == NS:
+            need("v", [v_eq, c_r16])
+            v_corr = done("v", V.tensor_tensor_scan(T.corr[:], T.reset16[:, 0:NT], T.eqw[:], 0.0, OP.mult, OP.add))
+        elif q == NS + 1:
+            need("v", [v_corr, c_slots])
+            v_first = done("v", V.tensor_scalar(T.first[:], T.corr[:, 15:NT:16], -1.0, -float(HALF), OP.mult, OP.add))
+            v_k = done("v", V.tensor_tensor(T.rk2[:], T.slots[:, 15:S0:16], T.corr[:, 15:S0:16], OP.subtract))
+        else:
+            k, d = late.pop(0)
+            total(k, [d, v_first])
+    k, d = late.pop(0)
+    total(k, [d])
+    need("v", [a_acc, v_k])
+    d0 = done("v", V.tensor_tensor(T.acc3[:], T.acc2[:], T.acc[:], OP.subtract))
+    k, d = late.pop(0)
+    v_sum = total(k, [d])
+    need("v", [d0])
+    d0 = done("v", V.tensor_tensor(T.rk[:], T.acc3[:], T.rk2[:], OP.add))
+    need("v", [v_sum])
+    done("v", V.tensor_scalar(T.offr[:, NS:NCMP], T.sums[:, HALF - 1:HALF * (NCMP - NS):HALF], float(HALF), None, OP.add))
+    need("v", [d0])
+    v_offr = done("v", V.tensor_copy(T.offr[:, 0:NS], T.rk[:]))
     need("v", [v_offr, c_tok])
     v_win = done("v", V.tensor_copy(T.win[:, 0:NT].indirect(T.offr[:, 0:NCMP]), T.tok[:]))
 
-    c_t1 = done("v", V.memset(T.t1[:, 96:128], 0.0))
-    need("v", [v_win])
+    need("v", [v_win, c_t1])
     v_t1 = done("v", V.transpose(T.t1[:, 0:96], T.win[:, 0:96]))
     need("v", [v_t1])
     v_t2 = done("v", V.transpose(T.t2[:, 0:96], T.t1[:, 16:112]))
     bc = {}
-    for e in order:
+
+    def spread(e):
         k = group_of[e]
         p0 = 32 * (k // 2)
         need("p", [v_win if k % 2 == 0 else v_t2])
         bc[e] = done("p", g.partition_broadcast(T.bl[:, CK * e:CK * e + CK], T["win" if k % 2 == 0 else "t2"][p0:p0 + 1, 0:CK], 128))
 
-    off = {}
+    for e in order[:-1]:
+        spread(e)
+    off, sel = {}, {}
 
-    def offsets(e):
+    def offsets(e, steps):
         c = slice(CK * e, CK * e + CK)
-        need("v", [bc[e], c_m4])
-        d = done("v", V.tensor_tensor(T.sel1[:, c], T.bl[:, c], T.mask4[:], OP.mult))
-        need("v", [d, c_r4])
-        d = done("v", V.tensor_tensor_scan(T.sel2[:, c], T.reset4[:, 0:CK], T.sel1[:, c], 0.0, OP.mult, OP.add))
-        need("v", [d])
-        off[e] = done("v", V.tensor_scalar(T.off4[:, 24 * e:24 * e + 24], T.sel2[:, CK * e + 3:CK * e + CK:4], T.p3[:, 0:1], None, OP.add))
+        for k in steps:
+            if k == "a":
+                need("v", [bc[e], c_m4])
+                sel[e] = done("v", V.tensor_tensor(T.sel1[:, c], T.bl[:, c], T.mask4[:], OP.mult))
+            elif k == "b":
+                need("v", [sel[e], c_r4])
+                sel[e] = done("v", V.tensor_tensor_scan(T.sel2[:, c], T.reset4[:, 0:CK], T.sel1[:, c], 0.0, OP.mult, OP.add))
+            else:
+                need("v", [sel[e]])
+                off[e] = done("v", V.tensor_scalar(T.off4[:, 24 * e:24 * e + 24], T.sel2[:, CK * e + 3:CK * e + CK:4], T.p3[:, 0:1], None, OP.add))
 
-    def gather(q, e):
-        out = T.xt[:, 4 * pos[e]:4 * pos[e] + 4 * CK]
-        win = T.xsb[:, 0:4 * NT].indirect(T.off4[:, 24 * e:24 * e + 24])
-        need(q, [off[e]])
+    def gather(q, e, lo=0, hi=24):
+        out = T.xt[:, 4 * pos[e] + 16 * lo:4 * pos[e] + 16 * hi]
+        win = T.xsb[:, 0:4 * NT].indirect(T.off4[:, 24 * e + lo:24 * e + hi])
+        need(q, [off[e], LDX, LDX2])
         return done(q, A.activation(out, win, AF.Copy) if q == "a" else V.tensor_copy(out, win))
 
     def pack(lo, hi, deps, src, qc, qs):
         need("v", deps)
         return done("v", V.quantize_mx(T[qc][:, lo:hi], T[qs][:, lo:hi], T[src][:, 4 * lo:4 * hi]))
-
-    for e in far:
-        offsets(e)
-    a_gf = [gather("a", e) for e in far[:2]][-1]
-    v_gf = gather("v", far[2])
-    v_qfar = pack(FAR0, NEAR0, [a_gf, v_gf], "xt", "ct", "cs")
-    offsets(near[0])
-    a_gn = gather("a", near[0])
-    offsets(near[1])
-    v_gn = gather("v", near[1])
-    v_qnear = pack(NEAR0, OWN0, [a_gn, v_gn], "xt", "ct", "cs")
-    offsets(me)
-    a_go = gather("a", me)
-    c_xpad = done("v", V.memset(T.xt[:, 4 * (OWN0 + CK):4 * ALLC], 0.0))
 
     local = [0]
 
@@ -227,14 +268,33 @@ def rank_program(g, core, T, topo):
                 local[0] += len(es)
             g.remote_dma_fused(tr, local_sem=T.sem["loc"])
 
-    send(True, v_qfar, "ct", "cs", "rxf", "rxfs", "df")
-    send(False, v_qnear, "ct", "cs", "rxn", "rxns", "dn")
     DF, DN, RF, RN = ("df", arrivals(True)), ("dn", arrivals(False)), ("rf", arrivals(True)), ("rn", arrivals(False))
 
-    need("v", [LDW])
-    for i in range(4):
-        v_qw = done("v", V.quantize_mx(T.qw[:, 128 * i:128 * i + 128], T.pw[:, 128 * i:128 * i + 128], T.w1s[:, 512 * i:512 * i + 512]))
-    v_qown = pack(OWN0, ALLC, [a_go, c_xpad], "xt", "ct", "cs")
+    for e in far:
+        offsets(e, "abc")
+    for e in far[:2]:
+        gather("a", e)
+    a_gf = gather("a", far[2], 12, 24)
+    v_gf = gather("v", far[2], 0, 12)
+    offsets(near[0], "a")
+    v_qfar = pack(FAR0, NEAR0, [a_gf, v_gf], "xt", "ct", "cs")
+    send(True, v_qfar, "ct", "cs", "rxf", "rxfs", "df")
+    spread(me)
+    offsets(near[1], "a")
+    offsets(near[0], "b")
+    offsets(near[1], "b")
+    offsets(near[0], "c")
+    offsets(near[1], "c")
+    a_gn = gather("a", near[0])
+    v_gn = gather("v", near[1])
+    offsets(me, "a")
+    v_qnear = pack(NEAR0, OWN0, [a_gn, v_gn], "xt", "ct", "cs")
+    send(False, v_qnear, "ct", "cs", "rxn", "rxns", "dn")
+    offsets(me, "bc")
+    need("a", [c_m16, bc[me]])
+    for m in range(16):
+        a_s16 = done("a", A.activation(T.s16[:, m:576:16], T.bl[:, m:576:16], AF.Copy, scale=T.mcol16[:, m:m + 1]))
+    a_go = gather("a", me)
 
     def products(stat, plane, codes, planes, lo, hi, bank, deps):
         need("t", deps)
@@ -263,65 +323,90 @@ def rank_program(g, core, T, topo):
         out, src = t[:, slot(e0) + b:slot(e0) + 4 * n:4], T.pp[:, o:o + n]
         return done(q, V.tensor_copy(out, src) if q == "v" else A.activation(out, src, AF.Copy))
 
-    need("v", [c_k4])
-    c_m16 = done("v", V.tensor_scalar(T.mcol16[:], T.k16[:, 0:16], T.p15[:, 0:1], None, OP.is_equal))
-    c_mcol = done("v", V.tensor_scalar(T.mcol[:], T.k4[:, 0:4], T.pm[:, 0:1], 4.0, OP.is_equal, OP.mult))
-    need("a", [c_m16, bc[order[-1]]])
-    for m in range(16):
-        a_s16 = done("a", A.activation(T.s16[:, m:576:16], T.bl[:, m:576:16], AF.Copy, scale=T.mcol16[:, m:m + 1]))
+    table = T.cl[:, NP:NP + NT]
+    tk = {"last": None}
 
-    p_own = products("qw", "pw", "ct", "cs", OWN0, ALLC, 0, [v_qw, v_qown, v_eq])
-    r1 = [relu("v", OWN0, ALLC, 0, i, p_own[i]) for i in (0, 1)]
-    r2 = [relu("a", OWN0, ALLC, 0, i, p_own[i]) for i in (2, 3)]
-    v_rown = pack(OWN0, ALLC, [r1[-1], r2[-1]], "rt", "rc", "rs")
-    need("v", [c_et])
-    for i in range(4):
-        v_qe = done("v", V.quantize_mx(T.qe[:, 128 * i:128 * i + 128], T.pe[:, 128 * i:128 * i + 128], T.et[:, 512 * i:512 * i + 512]))
-    c_cl = done("v", V.memset(T.cl[:, 0:NT], 0.0))
-    c_aa = done("v", V.memset(T.aa[:, 0:4], 0.0))
+    def tab(k):
+        e = (k + 1) // 2
+        o16 = T.off16[:, 6 * e:6 * e + 6]
+        need("v", [tk["last"]])
+        if k % 2:
+            tk["last"] = done("v", V.tensor_copy(T.cl[:, CK * (e - 1):CK * e], table.indirect(o16)))
+            if e == N - 1:
+                mask(0, NP)
+        else:
+            tk["last"] = done("v", V.tensor_copy(table.indirect(o16), T.slots[:, CK * e:CK * e + CK]))
+
+    def mask(lo, hi):
+        need("a", [tk["last"], c_mcol])
+        for m in range(4):
+            tk[lo] = done("a", A.activation(T.cm[:, lo + m:hi:4], T.cl[:, lo + m:hi:4], AF.Copy, scale=T.mcol[:, m:m + 1]))
+
+    def wrap(lo, hi):
+        need("v", [tk[lo], c_r4])
+        d = done("v", V.tensor_tensor_scan(T.cq[:, lo:hi], T.reset4[:, lo:hi], T.cm[:, lo:hi], 0.0, OP.mult, OP.add))
+        need("v", [d])
+        return done("v", V.tensor_scalar(T.offc[:, lo // 4:hi // 4], T.cq[:, lo + 3:hi:4], T.p3[:, 0:1], None, OP.add))
+
+    def qweight(i):
+        need("v", [LDW])
+        return done("v", V.quantize_mx(T.qw[:, 128 * i:128 * i + 128], T.pw[:, 128 * i:128 * i + 128], T.w1s[:, 512 * i:512 * i + 512]))
+
+    def qunpack(i):
+        need("v", [c_et])
+        return done("v", V.quantize_mx(T.qe[:, 128 * i:128 * i + 128], T.pe[:, 128 * i:128 * i + 128], T.et[:, 512 * i:512 * i + 512]))
+
+    qweight(0)
+    qweight(1)
     need("v", [a_s16])
     d = done("v", V.tensor_tensor_scan(T.s16b[:], T.reset16[:], T.s16[:], 0.0, OP.mult, OP.add))
+    qweight(2)
     need("v", [d])
     v_o16 = done("v", V.tensor_copy(T.off16[:], T.s16b[:, 15:576:16]))
+    v_qw = qweight(3)
+    need("v", [v_o16, c_cl, c_slots])
+    tab(0)
+    v_qown = pack(OWN0, ALLC, [a_go, c_xpad], "xt", "ct", "cs")
+    tab(1)
+    qunpack(0)
+    tab(2)
+    qunpack(1)
+    tab(3)
+    p_own = products("qw", "pw", "ct", "cs", OWN0, ALLC, 0, [v_qw, v_qown, v_eq, a_acc])
+    r1 = [relu("v", OWN0, ALLC, 0, i, p_own[i]) for i in (0, 1)]
+    r2 = [relu("a", OWN0, ALLC, 0, i, p_own[i]) for i in (2, 3)]
+    tab(4)
+    v_rown = pack(OWN0, ALLC, [r1[-1], r2[-1]], "rt", "rc", "rs")
 
     p_far = products("qw", "pw", "rxf", "rxfs", 0, 288, 4, [DF])
-    f1 = [relu("v", FAR0, NEAR0, 4, i, p_far[i]) for i in (0, 1)]
-    f2 = [relu("a", FAR0, NEAR0, 4, i, p_far[i]) for i in (2, 3)]
+    f1 = [relu("v", FAR0, NEAR0, 4, i, p_far[i]) for i in (0, 2)]
+    f2 = [relu("a", FAR0, NEAR0, 4, i, p_far[i]) for i in (1, 3)]
     v_rfar = pack(FAR0, NEAR0, [f1[-1], f2[-1]], "rt", "rc", "rs")
     send(True, v_rfar, "rc", "rs", "bkf", "bkfs", "rf")
+    qunpack(2)
+    v_qe = qunpack(3)
 
     p_near = products("qw", "pw", "rxn", "rxns", 0, 192, 0, [DN, r1[-1], r2[-1]])
-    e_near = [relu("a", NEAR0, OWN0, 0, i, p_near[i]) for i in range(4)]
-    v_rnear = pack(NEAR0, OWN0, [e_near[-1]], "rt", "rc", "rs")
+    e_near = [relu("va"[i % 2], NEAR0, OWN0, 0, i, p_near[i]) for i in range(4)][2:]
+    v_rnear = pack(NEAR0, OWN0, e_near, "rt", "rc", "rs")
     send(False, v_rnear, "rc", "rs", "bkn", "bkns", "rn")
 
     u_own = products("qe", "pe", "rc", "rs", OWN0, ALLC, 4, [v_rown, v_qe, f1[-1], f2[-1]])
     d_own = [unpack("a", me, CK, 4, 0, b, u_own[b]) for b in range(4)]
 
-    last = None
-    need("v", [v_o16, c_cl, c_slots])
-    for e in range(N):
-        o16 = T.off16[:, 6 * e:6 * e + 6]
-        need("v", [last])
-        if e:
-            last = done("v", V.tensor_copy(T.cl[:, NT + CK * (e - 1):NT + CK * e], T.cl[:, 0:NT].indirect(o16)))
-            need("v", [last])
-        last = done("v", V.tensor_copy(T.cl[:, 0:NT].indirect(o16), T.slots[:, CK * e:CK * e + CK]))
-    need("a", [last, c_mcol])
-    for m in range(4):
-        a_cm = done("a", A.activation(T.cm[:, m:864:4], T.cl[:, m:864:4], AF.Copy, scale=T.mcol[:, m:m + 1]))
-    need("v", [a_cm, c_r4])
-    d = done("v", V.tensor_tensor_scan(T.cq[:], T.reset4[:], T.cm[:], 0.0, OP.mult, OP.add))
-    need("v", [d])
-    v_offc = done("v", V.tensor_scalar(T.offc[:], T.cq[:, 3:864:4], T.p3[:, 0:1], None, OP.add))
+    for k in range(5, 2 * N - 1):
+        tab(k)
+    v_prev = wrap(0, NP)
+    mask(NP, NP + NT)
+    v_last = wrap(NP, NP + NT)
 
-    u_near = products("qe", "pe", "bkn", "bkns", 0, 192, 0, [RN, e_near[-1]])
+    u_near = products("qe", "pe", "bkn", "bkns", 0, 192, 0, [RN] + e_near)
     d_near = [unpack("a", near[i], CK, 0, CK * i, b, u_near[b]) for b in range(4) for i in range(2)]
     u_far = products("qe", "pe", "bkf", "bkfs", 0, 288, 4, [RF, d_own[-1]])
 
     def chain(e, deps):
-        need("v", deps + [v_offc, c_aa])
-        o = 96 + 24 * (e - 1)
+        need("v", deps + [v_prev, c_aa])
+        o = 24 * (e - 1)
         s = slice(slot(e), slot(e) + 4 * CK)
         return done("v", V.tensor_tensor(T.aa[:, s], T.aa[:, 0:slot(e)].indirect(T.offc[:, o:o + 24]), T.dd[:, s], OP.add))
 
@@ -341,18 +426,18 @@ def rank_program(g, core, T, topo):
     for e in range(1 if far[0] == 0 else 3, N):
         step = chain(e, dlast + [d1, d2, step])
 
-    H = NT
     win = T.aa[:, 0:slot(N)]
     for q, quarters in (("v", (0, 1)), ("a", (2, 3))):
-        need(q, [step, v_offc])
+        need(q, [step, v_last])
         r = []
         for k in quarters:
-            out, src = T.yy[:, H * k:H * k + H], win.indirect(T.offc[:, 24 * k:24 * k + 24])
+            o = NP // 4 + 24 * k
+            out, src = T.yy[:, NT * k:NT * k + NT], win.indirect(T.offc[:, o:o + 24])
             r.append(done(q, V.tensor_copy(out, src) if q == "v" else A.activation(out, src, AF.Copy)))
         dq, sem = ("s", "sty") if q == "v" else ("a", "sty2")
         for k, d in zip(quarters, r):
             need(dq, [d])
-            Q[dq][0].dma_start(T.y[:, H * k:H * k + H], T.yy[:, H * k:H * k + H]).then_inc(T.sem[sem], 16)
+            Q[dq][0].dma_start(T.y[:, NT * k:NT * k + NT], T.yy[:, NT * k:NT * k + NT]).then_inc(T.sem[sem], 16)
 
     g.wait_ge(T.sem["loc"], local[0])
     for s in count:

@@ -8,24 +8,29 @@ BIG = 1e29
 F8, U8, F32, BF, U16, I32 = "float8_e4m3fn_x4", "uint8", "float32", "bfloat16", "uint16", "int32"
 
 FAR0, NEAR0, OWN0, ALLC = 0, 3 * CK, 5 * CK, 5 * CK + 128
-NCMP = NT // 16
-NS = 9
-S0 = 16 * NS
 HALF = NT // 2
 NP = CK * (N - 1)
+ROUNDS = ({"k": "1", "W": 32, "NS": 5, "bank": 0}, {"k": "2", "W": 64, "NS": 3, "bank": 2})
 
 SHAPES = {
-    BF: {"xsb": 4 * NT, "wgs": 32, "wga": 512, "w1s": 2048, "ones": 512, "et": 2048, "reset16": 576, "reset4": 864,
-         "cmp": NCMP * NT, "sums": (NCMP - NS) * HALF, "eqw": NT, "corr": NT, "xt": 4 * ALLC, "rt": 4 * ALLC},
-    F8: {"qx": NT, "qg": 128, "qw": 512, "qe": 512, "ct": ALLC, "rxn": 192, "rxf": 288, "rc": ALLC, "bkn": 192, "bkf": 288},
-    U8: {"px": NT, "pg": 128, "pw": 512, "pe": 512, "cs": ALLC, "rxns": 192, "rxfs": 288, "rs": ALLC, "bkns": 192, "bkfs": 288},
-    I32: {"pi": 2, "p3i": 2, "p15i": 2, "pmi": 2},
-    U16: {"offw": 32, "offr": NCMP, "off4": 144, "off16": 36, "offc": 216},
-    F32: {"p3": 2, "p15": 2, "pm": 2, "offwf": 32, "k16": 576, "k4": 864, "tok": NT, "slots": 576, "m3": NT, "rr": NT,
-          "mask4": CK, "mcol": 4, "mcol16": 16, "md": NT, "sc": NT, "acc": NS, "acc2": NS, "acc3": NS, "rk": NS, "rk2": NS,
-          "first": NCMP, "win": NT, "t1": 128, "t2": 96, "bl": 576, "sel1": 576, "sel2": 576, "s16": 576, "s16b": 576,
-          "cl": NP + NT, "cm": NP + NT, "cq": NP + NT, "dd": 8 + 4 * 576, "aa": 8 + 4 * 576, "yy": 4 * NT},
+    BF: {"xsb": 4 * NT, "wgs": 32, "wga1": 512, "wga2": 512, "w1s": 2048, "ones": 512, "et": 2048, "reset1": NT, "reset2": NT,
+         "reset4": NP, "xt": 4 * ALLC, "rt": 4 * ALLC},
+    F8: {"qx": NT, "qg1": 128, "qg2": 128, "qw": 512, "qe": 512, "ct": ALLC, "rxn": 192, "rxf": 288, "rc": ALLC, "bkn": 192, "bkf": 288},
+    U8: {"px": NT, "pg1": 128, "pg2": 128, "pw": 512, "pe": 512, "cs": ALLC, "rxns": 192, "rxfs": 288, "rs": ALLC, "bkns": 192, "bkfs": 288},
+    I32: {"pi": 2, "pci": 8},
+    U16: {"offw": 64, "off4": 144, "off16": 36, "offc": 216},
+    F32: {"pc": 8, "offwf": 64, "k1": NT, "k2": NT, "im4": 32, "im16": 32, "k4s": CK, "k16s": CK, "k4": NP, "cut1": 12, "cut2": 6,
+          "slots": 576, "mask4": 32, "mask16": 32, "rr4": CK, "rr16": CK, "mcol": 4, "v2": 6, "offf": 36,
+          "cl": NP + NT, "cm": NP + NT, "cq": NP + NT, "aa": 8 + 4 * 576, "yy": 4 * NT},
 }
+for R in ROUNDS:
+    k, n, ns = R["k"], NT // R["W"], R["NS"]
+    R["n"] = n
+    SHAPES[BF].update({"cmp" + k: n * NT, "sums" + k: (n - ns) * HALF, "eqw" + k: NT, "corr" + k: NT})
+    SHAPES[U16].update({"offr" + k: n})
+    SHAPES[F32].update({"m3" + k: NT, "rr" + k: NT, "md" + k: NT, "sc" + k: NT, "acc" + k: ns, "accb" + k: ns, "accc" + k: ns, "rk" + k: ns, "rkb" + k: ns,
+                        "first" + k: n, "tok" + k: 16 * n, "tokf" + k: 16 * n, "win" + k: NT, "t1" + k: CK, "wa" + k: CK, "t2" + k: CK, "s4" + k: CK,
+                        "wb" + k: CK, "t3" + k: CK, "s16" + k: CK})
 SCRATCH = {name: ("sbuf", [128, n], kind) for kind in SHAPES for name, n in SHAPES[kind].items()}
 SCRATCH["pp"] = ("psum", [128, 4096], F32)
 SEMAPHORES = ["sv", "sa", "sten", "sp", "ldx", "ldx2", "ldg", "ldw", "sty", "sty2", "loc", "dn", "df", "rn", "rf"]
@@ -45,11 +50,8 @@ def rank_program(g, core, T, topo):
 
     far, near = far_of(me), near_of(me)
     order = far + near + [me]
-    group_of = {e: (0, 2, 4, 6, 1, 3)[i] for i, e in enumerate(order)}
-    expert_of = [far[0]] * 8
-    for e in order:
-        expert_of[group_of[e]] = e
-    pos = {e: CK * i for i, e in enumerate(order)}
+    idx = {e: i for i, e in enumerate(order)}
+    pos = {e: CK * idx[e] for e in order}
 
     Q = {"v": (g.vector, "sv"), "a": (g.scalar, "sa"), "t": (g.tensor, "sten"), "p": (g, "sp"), "s": (g.sync, None)}
     count = {"sv": 0, "sa": 0, "sten": 0, "sp": 0}
@@ -77,158 +79,255 @@ def rank_program(g, core, T, topo):
     g.sync.dma_start(T.w1s[:], T.w1[:]).then_inc(T.sem["ldw"], 16)
     LDX, LDX2, LDG, LDW = ("ldx", 16), ("ldx2", 16), ("ldg", 16), ("ldw", 16)
 
-    def iota(name, pattern, base, cm):
+    def iota(name, pattern, base=0, cm=0):
         if name == "pi":
             return done("p", g.iota(T.pi[:], pattern, base, cm))
         return done("p", g.iota(T[name][:], pattern, base, cm, allow_small_or_imprecise_dtypes=True))
 
     c_pi = iota("pi", [[0, 2]], 0, 1)
-    c_k16 = iota("k16", [[0, 36], [1, 16]], 0, 0)
-    c_k4 = iota("k4", [[0, 216], [1, 4]], 0, 0)
-    c_tok = iota("tok", [[1, NT]], 0, 0)
-    c_slots = iota("slots", [[1, 576]], 1, 0)
+    c_k = {"1": iota("k1", [[0, 12], [1, 32]])}
+    c_im4 = iota("im4", [[0, 2], [1, 4], [0, 4]])
+    c_im16 = iota("im16", [[0, 2], [1, 16]])
+    c_k4s = iota("k4s", [[0, 24], [1, 4]])
+    c_k16s = iota("k16s", [[0, 6], [1, 16]])
+    c_cut = {"1": iota("cut1", [[32, 12]], 32)}
+    c_k["2"] = iota("k2", [[0, 6], [1, 64]])
+    c_tokf = {"1": iota("tokf1", [[32, 12], [1, 16]]), "2": iota("tokf2", [[64, 6], [1, 16]])}
+    c_cut["2"] = iota("cut2", [[64, 6]], 64)
+    c_slots = iota("slots", [[1, 576]], 1)
+    c_k4 = iota("k4", [[0, NP // 4], [1, 4]])
 
-    for k in range(8):
-        c_off = done("v", V.memset(T.offwf[:, 4 * k:4 * k + 4], float(4 * expert_of[k])))
-    need("v", [c_pi])
-    c_p3i = done("v", V.tensor_scalar(T.p3i[:], T.pi[:], 3, None, OP.bitwise_and))
-    c_p15i = done("v", V.tensor_scalar(T.p15i[:], T.pi[:], 15, None, OP.bitwise_and))
-    c_pmi = done("v", V.tensor_scalar(T.pmi[:], T.pi[:], 15, 2, OP.bitwise_and, OP.logical_shift_right))
-    need("v", [c_p3i])
-    c_p3 = done("v", V.tensor_copy(T.p3[:], T.p3i[:]))
-    need("v", [c_p15i, c_pmi])
-    c_p15 = done("v", V.tensor_copy(T.p15[:], T.p15i[:]))
-    c_pm = done("v", V.tensor_copy(T.pm[:], T.pmi[:]))
-    need("v", [c_off, c_p3])
-    c_offw = done("v", V.tensor_scalar(T.offw[:], T.offwf[:], T.p3[:, 0:1], None, OP.add))
-    need("v", [c_k16, c_pm])
-    c_m3 = done("v", V.tensor_scalar(T.m3[:], T.k16[:, 0:NT], T.p15[:, 0:1], -BIG, OP.not_equal, OP.mult))
+    for i in range(4):
+        done("v", V.memset(T.offwf[:, 8 * i:8 * i + 8], float(4 * order[i])))
+    for i in (4, 5):
+        c_offwf = done("v", V.memset(T.offwf[:, 16 * i - 32:16 * i - 16], float(4 * order[i])))
     c_ones = done("v", V.memset(T.ones[:], 1.0))
-    c_t1 = done("v", V.memset(T.t1[:, 96:128], 0.0))
+    P3, P15, W31, W63, H16, H48, PM = range(7)
+    need("v", [c_pi])
+    for k, m in enumerate((3, 15, 31, 63, 16, 48)):
+        done("v", V.tensor_scalar(T.pci[:, k:k + 1], T.pi[:, 0:1], m, None, OP.bitwise_and))
+    done("v", V.tensor_scalar(T.pci[:, PM:PM + 1], T.pi[:, 0:1], 15, 2, OP.bitwise_and, OP.logical_shift_right))
+    d = done("v", V.tensor_scalar(T.pci[:, 7:8], T.pi[:, 0:1], 0, None, OP.bitwise_and))
+    c_win = [done("v", V.memset(T[w][:, 0:CK], 0.0)) for w in ("win1", "win2")][-1]
+    need("v", [d])
+    c_pc = done("v", V.tensor_copy(T.pc[:], T.pci[:]))
+    c_v2 = done("v", V.memset(T.v2[:], 0.0))
+
+    def pcol(k, lo=0, hi=128):
+        return T.pc[lo:hi, k:k + 1]
+
+    need("v", [c_offwf, c_pc])
+    c_offw = done("v", V.tensor_scalar(T.offw[:], T.offwf[:], pcol(P3), None, OP.add))
+    c_m3 = {}
+
+    def m3(k, col):
+        need("v", [c_k[k]])
+        c_m3[k] = done("v", V.tensor_scalar(T["m3" + k][:], T["k" + k][:], pcol(col), -BIG, OP.not_equal, OP.mult))
+
+    m3("1", W31)
     c_xpad = done("v", V.memset(T.xt[:, 4 * (OWN0 + CK):4 * ALLC], 0.0))
-    c_cl = done("v", V.memset(T.cl[:, NP:NP + NT], 0.0))
     c_aa = done("v", V.memset(T.aa[:, 0:4], 0.0))
 
-    need("a", [c_k16])
-    c_r16 = done("a", A.activation(T.reset16[:], T.k16[:], AF.Sign))
-    need("a", [c_offw, LDG])
-    a_wga = done("a", A.activation(T.wga[:], T.wgs[:, 0:32].indirect(T.offw[:, 0:32]), AF.Copy))
-    need("a", [c_r16])
-    c_rr = done("a", A.activation(T.rr[:], T.reset16[:, 0:NT], AF.Copy, bias=-BIG, scale=BIG))
-    need("a", [c_k4])
-    c_r4 = done("a", A.activation(T.reset4[:], T.k4[:], AF.Sign))
+    c_reset, c_rr, c_tok, a_wga = {}, {}, {}, {}
+
+    def reset(k):
+        need("a", [c_k[k]])
+        c_reset[k] = done("a", A.activation(T["reset" + k][:], T["k" + k][:], AF.Sign))
+
+    def rr(k):
+        need("a", [c_reset[k]])
+        c_rr[k] = done("a", A.activation(T["rr" + k][:], T["reset" + k][:], AF.Copy, bias=-BIG, scale=BIG))
+
+    def tokens(k, col):
+        need("a", [c_tokf[k], c_pc])
+        c_tok[k] = done("a", A.activation(T["tok" + k][:], T["tokf" + k][:], AF.Identity, bias=pcol(col)))
+
+    def gates(k, lo):
+        need("a", [c_offw, LDG])
+        a_wga[k] = done("a", A.activation(T["wga" + k][:], T.wgs[:, 0:32].indirect(T.offw[:, lo:lo + 32]), AF.Copy))
+
+    reset("1")
+    gates("1", 0)
+    rr("1")
+    gates("2", 32)
+    tokens("1", H16)
+    reset("2")
+    tokens("2", H48)
 
     need("p", [c_ones])
-    for b in range(4):
-        c_et = done("p", g.affine_select(T.et[:, 512 * b:512 * b + 512], T.ones[:], [[-1, 512]], OP.is_equal, 0.0, b, 4))
 
-    need("v", [a_wga])
-    v_qg = done("v", V.quantize_mx(T.qg[:], T.pg[:], T.wga[:]))
+    def one_tile(b):
+        return done("p", g.affine_select(T.et[:, 512 * b:512 * b + 512], T.ones[:], [[-1, 512]], OP.is_equal, 0.0, b, 4))
+
+    c_et = [one_tile(0), one_tile(1)]
+
+    need("v", [a_wga["1"]])
+    done("v", V.quantize_mx(T.qg1[:], T.pg1[:], T.wga1[:]))
     need("v", [LDX])
     done("v", V.quantize_mx(T.qx[:, 0:HALF], T.px[:, 0:HALF], T.xsb[:, 0:4 * HALF]))
+    need("v", [c_im4, c_im16, c_k4s, c_k16s])
+    done("v", V.tensor_scalar(T.mask4[:], T.im4[:], pcol(P3), -BIG, OP.not_equal, OP.mult))
+    done("v", V.tensor_scalar(T.mask16[:], T.im16[:], pcol(P15), -BIG, OP.not_equal, OP.mult))
+    done("v", V.tensor_scalar(T.mcol[:], T.k4s[:, 0:4], pcol(PM), 4.0, OP.is_equal, OP.mult))
+    done("v", V.tensor_scalar(T.rr4[:], T.k4s[:], 0.0, -BIG, OP.is_equal, OP.mult))
+    c_lists = done("v", V.tensor_scalar(T.rr16[:], T.k16s[:], 0.0, -BIG, OP.is_equal, OP.mult))
     need("v", [LDX2])
     v_qx = done("v", V.quantize_mx(T.qx[:, HALF:NT], T.px[:, HALF:NT], T.xsb[:, 4 * HALF:4 * NT]))
-    need("t", [v_qg, v_qx])
-    t_z, t_z2 = [done("t", TE.matmul_mx(T.pp[:, 512 * k:512 * k + NT], T.qg[:], T.pg[:], T.qx[:], T.px[:], True, True)) for k in (0, 1)]
-    Z, Z2 = T.pp[:, 0:NT], T.pp[:, 512:512 + NT]
-    need("v", [c_k4])
-    c_m4 = done("v", V.tensor_scalar(T.mask4[:], T.k4[:, 0:CK], T.pm[:, 0:1], 4.0, OP.is_equal, OP.mult))
-    c_m16 = done("v", V.tensor_scalar(T.mcol16[:], T.k16[:, 0:16], T.p15[:, 0:1], None, OP.is_equal))
-    c_mcol = done("v", V.tensor_scalar(T.mcol[:], T.k4[:, 0:4], T.pm[:, 0:1], 4.0, OP.is_equal, OP.mult))
+    m3("2", W63)
+    need("v", [a_wga["2"]])
+    v_qg2 = done("v", V.quantize_mx(T.qg2[:], T.pg2[:], T.wga2[:]))
+    t_z = {}
+    for R, dep in zip(ROUNDS, (v_qx, v_qg2)):
+        k = R["k"]
+        need("t", [dep])
+        t_z[k] = [done("t", TE.matmul_mx(T.pp[:, 512 * b:512 * b + NT], T["qg" + k][:], T["pg" + k][:], T.qx[:], T.px[:], True, True)) for b in (R["bank"], R["bank"] + 1)]
 
-    parts = ((0, S0), (S0, NT))
-    need("v", [t_z, c_m3])
-    v_md = [done("v", V.tensor_tensor(T.md[:, lo:hi], T.pp[:, lo:hi], T.m3[:, lo:hi], OP.add)) for lo, hi in parts]
-    v_sc = []
-    for (lo, hi), d in zip(parts, v_md):
-        need("v", [d, c_rr])
-        v_sc.append(done("v", V.tensor_tensor_scan(T.sc[:, lo:hi], T.rr[:, lo:hi], T.md[:, lo:hi], 0.0, OP.add, OP.max)))
+    def z(R, other, lo=0, hi=NT):
+        o = 512 * (R["bank"] + other)
+        return T.pp[:, o + lo:o + hi]
 
-    need("a", [t_z2, v_sc[0]])
-    signs = []
-    for q in range(NS + 1):
-        if q < NS:
-            signs.append(done("a", A.activation(T.cmp[:, NT * q:NT * q + NT], Z2, AF.Sign, bias=T.sc[:, 16 * q + 15:16 * q + 16], scale=-1.0)))
-        if q:
-            k, c = q - 1, NT * (q - 1)
-            lower, higher = T.cmp[:, c:c + 16 * q], T.cmp[:, c + 16 * q:c + NT]
-            need("a", [signs[k]])
-            done("a", A.activation(lower, lower, AF.Relu, accum_out=T.acc[:, k:k + 1]))
-            a_acc = done("a", A.activation(higher, higher, AF.Relu, scale=-1.0, accum_out=T.acc2[:, k:k + 1]))
+    v_sc = {}
 
-    def total(q, deps):
-        o, c = HALF * (q - NS), NT * q
-        need("v", deps)
-        return done("v", V.tensor_tensor_scan(T.sums[:, o:o + HALF], T.cmp[:, c:c + HALF], T.cmp[:, c + HALF:c + NT], T.first[:, q:q + 1], OP.add, OP.add))
+    def own_mask(R, lo, hi):
+        k = R["k"]
+        need("v", [t_z[k][0], c_m3[k]])
+        return done("v", V.tensor_tensor(T["md" + k][:, lo:hi], z(R, 0, lo, hi), T["m3" + k][:, lo:hi], OP.add))
 
-    need("v", [v_sc[1]])
-    v_eq = done("v", V.tensor_tensor(T.eqw[:], Z, T.sc[:], OP.is_equal))
-    late = []
-    for q in range(NS, NCMP):
-        s = T.sc[:, 16 * q + 15:16 * q + 16]
-        cut, c = 16 * q + 16, NT * q
-        d = done("v", V.tensor_scalar(T.cmp[:, c:c + cut], T.pp[:, 0:cut], s, None, OP.is_ge))
-        if cut < NT:
-            d = done("v", V.tensor_scalar(T.cmp[:, c + cut:c + NT], T.pp[:, cut:NT], s, None, OP.is_gt))
-        late.append((q, d))
-        if q == NS:
-            need("v", [v_eq, c_r16])
-            v_corr = done("v", V.tensor_tensor_scan(T.corr[:], T.reset16[:, 0:NT], T.eqw[:], 0.0, OP.mult, OP.add))
-        elif q == NS + 1:
-            need("v", [v_corr, c_slots])
-            v_first = done("v", V.tensor_scalar(T.first[:], T.corr[:, 15:NT:16], -1.0, -float(HALF), OP.mult, OP.add))
-            v_k = done("v", V.tensor_tensor(T.rk2[:], T.slots[:, 15:S0:16], T.corr[:, 15:S0:16], OP.subtract))
-        else:
-            k, d = late.pop(0)
-            total(k, [d, v_first])
-    k, d = late.pop(0)
-    total(k, [d])
-    need("v", [a_acc, v_k])
-    d0 = done("v", V.tensor_tensor(T.acc3[:], T.acc2[:], T.acc[:], OP.subtract))
-    k, d = late.pop(0)
-    v_sum = total(k, [d])
-    need("v", [d0])
-    d0 = done("v", V.tensor_tensor(T.rk[:], T.acc3[:], T.rk2[:], OP.add))
-    need("v", [v_sum])
-    done("v", V.tensor_scalar(T.offr[:, NS:NCMP], T.sums[:, HALF - 1:HALF * (NCMP - NS):HALF], float(HALF), None, OP.add))
-    need("v", [d0])
-    v_offr = done("v", V.tensor_copy(T.offr[:, 0:NS], T.rk[:]))
-    need("v", [v_offr, c_tok])
-    v_win = done("v", V.tensor_copy(T.win[:, 0:NT].indirect(T.offr[:, 0:NCMP]), T.tok[:]))
+    def own_scan(R, lo, hi, dep):
+        k = R["k"]
+        need("v", [dep, c_rr[k]])
+        v_sc[k + str(lo)] = done("v", V.tensor_tensor_scan(T["sc" + k][:, lo:hi], T["rr" + k][:, lo:hi], T["md" + k][:, lo:hi], 0.0, OP.add, OP.max))
 
-    need("v", [v_win, c_t1])
-    v_t1 = done("v", V.transpose(T.t1[:, 0:96], T.win[:, 0:96]))
-    need("v", [v_t1])
-    v_t2 = done("v", V.transpose(T.t2[:, 0:96], T.t1[:, 16:112]))
-    bc = {}
+    a_acc = {}
 
-    def spread(e):
-        k = group_of[e]
-        p0 = 32 * (k // 2)
-        need("p", [v_win if k % 2 == 0 else v_t2])
-        bc[e] = done("p", g.partition_broadcast(T.bl[:, CK * e:CK * e + CK], T["win" if k % 2 == 0 else "t2"][p0:p0 + 1, 0:CK], 128))
+    def scalar_ranks(R):
+        k, W, ns = R["k"], R["W"], R["NS"]
+        need("a", [t_z[k][1], v_sc[k + "0"]])
+        cmp, signs = T["cmp" + k], []
+        for q in range(ns + 1):
+            if q < ns:
+                signs.append(done("a", A.activation(cmp[:, NT * q:NT * q + NT], z(R, 1), AF.Sign, bias=T["sc" + k][:, W * q + W - 1:W * q + W], scale=-1.0)))
+            if q:
+                j, c = q - 1, NT * (q - 1)
+                lower, higher = cmp[:, c:c + W * q], cmp[:, c + W * q:c + NT]
+                need("a", [signs[j]])
+                done("a", A.activation(lower, lower, AF.Relu, accum_out=T["acc" + k][:, j:j + 1]))
+                a_acc[k] = done("a", A.activation(higher, higher, AF.Relu, scale=-1.0, accum_out=T["accb" + k][:, j:j + 1]))
 
-    for e in order[:-1]:
-        spread(e)
-    off, sel = {}, {}
+    v_eq = {}
 
-    def offsets(e, steps):
-        c = slice(CK * e, CK * e + CK)
-        for k in steps:
-            if k == "a":
-                need("v", [bc[e], c_m4])
-                sel[e] = done("v", V.tensor_tensor(T.sel1[:, c], T.bl[:, c], T.mask4[:], OP.mult))
-            elif k == "b":
-                need("v", [sel[e], c_r4])
-                sel[e] = done("v", V.tensor_tensor_scan(T.sel2[:, c], T.reset4[:, 0:CK], T.sel1[:, c], 0.0, OP.mult, OP.add))
+    def vector_ranks(R, fill):
+        k, W, ns, n = R["k"], R["W"], R["NS"], R["n"]
+        cmp, sc, corr, first, offr = T["cmp" + k], T["sc" + k], T["corr" + k], T["first" + k], T["offr" + k]
+        s0 = W * ns
+
+        def total(q, deps):
+            o, c = HALF * (q - ns), NT * q
+            need("v", deps)
+            return done("v", V.tensor_tensor_scan(T["sums" + k][:, o:o + HALF], cmp[:, c:c + HALF], cmp[:, c + HALF:c + NT], first[:, q:q + 1], OP.add, OP.add))
+
+        need("v", [v_sc[k + str(s0)]])
+        v_eq[k] = done("v", V.tensor_tensor(T["eqw" + k][:], z(R, 0), sc[:], OP.is_equal))
+        late = []
+        for q in range(ns, n):
+            s = sc[:, W * q + W - 1:W * q + W]
+            cut, c = W * q + W, NT * q
+            d = done("v", V.tensor_scalar(cmp[:, c:c + cut], z(R, 0, 0, cut), s, None, OP.is_ge))
+            if cut < NT:
+                d = done("v", V.tensor_scalar(cmp[:, c + cut:c + NT], z(R, 0, cut, NT), s, None, OP.is_gt))
+            late.append((q, d))
+            if q == ns:
+                need("v", [v_eq[k], c_reset[k]])
+                v_corr = done("v", V.tensor_tensor_scan(corr[:], T["reset" + k][:], T["eqw" + k][:], 0.0, OP.mult, OP.add))
+            elif q == ns + 1:
+                need("v", [v_corr, c_cut[k]])
+                v_first = done("v", V.tensor_scalar(first[:], corr[:, W - 1:NT:W], -1.0, -float(HALF), OP.mult, OP.add))
+                v_k = done("v", V.tensor_tensor(T["rkb" + k][:], T["cut" + k][:, 0:ns], corr[:, W - 1:s0:W], OP.subtract))
             else:
-                need("v", [sel[e]])
-                off[e] = done("v", V.tensor_scalar(T.off4[:, 24 * e:24 * e + 24], T.sel2[:, CK * e + 3:CK * e + CK:4], T.p3[:, 0:1], None, OP.add))
+                j, d = late.pop(0)
+                total(j, [d, v_first])
+        j, d = late.pop(0)
+        total(j, [d, v_first])
+        need("v", [a_acc[k], v_k])
+        d0 = done("v", V.tensor_tensor(T["accc" + k][:], T["accb" + k][:], T["acc" + k][:], OP.subtract))
+        j, d = late.pop(0)
+        v_sum = total(j, [d])
+        need("v", [d0])
+        d0 = done("v", V.tensor_tensor(T["rk" + k][:], T["accc" + k][:], T["rkb" + k][:], OP.add))
+        need("v", [v_sum])
+        done("v", V.tensor_scalar(offr[:, ns:n], T["sums" + k][:, HALF - 1:HALF * (n - ns):HALF], float(HALF), None, OP.add))
+        need("v", [d0])
+        v_offr = done("v", V.tensor_copy(offr[:, 0:ns], T["rk" + k][:]))
+        fill()
+        need("v", [v_offr, c_tok[k], c_win])
+        return done("v", V.tensor_copy(T["win" + k][:, 0:NT].indirect(offr[:, 0:n]), T["tok" + k][:]))
 
-    def gather(q, e, lo=0, hi=24):
-        out = T.xt[:, 4 * pos[e] + 16 * lo:4 * pos[e] + 16 * hi]
-        win = T.xsb[:, 0:4 * NT].indirect(T.off4[:, 24 * e + lo:24 * e + hi])
-        need(q, [off[e], LDX, LDX2])
+    v_t3, v_s16, off = {}, {}, {}
+
+    def lists(R, v_win, fill):
+        k = R["k"]
+        t1 = T["t1" + k]
+        fill()
+        need("v", [v_win, c_lists])
+        d = done("v", V.transpose(t1[:], T["win" + k][:, 0:CK]))
+        fill()
+        need("v", [d])
+        if k == "1":
+            pair = [(t1[:, 32 * u:32 * u + 1], t1[:, 32 * u + 16:32 * u + 17]) for u in range(3)]
+        else:
+            for b in (0, 64):
+                d = done("v", V.tensor_tensor(T.v2[b:b + 32, :], t1[b:b + 32, 0:CK:16], t1[b + 32:b + 64, 0:CK:16], OP.add))
+            pair = [(T.v2[:, 2 * u:2 * u + 1], T.v2[:, 2 * u + 1:2 * u + 2]) for u in range(3)]
+            fill()
+            need("v", [d, c_v2])
+
+        def under(w, mask, u):
+            return done("v", V.tensor_scalar(T[w + k][:, 32 * u:32 * u + 32], T[mask][:], pair[u][0], pair[u][1], OP.add, OP.add))
+
+        d = [under("wa", "mask4", u) for u in range(3)][-1]
+        under("wb", "mask16", 0)
+        need("v", [d])
+        d = done("v", V.transpose(T["t2" + k][:], T["wa" + k][:]))
+        under("wb", "mask16", 1)
+        need("v", [d])
+        d = done("v", V.tensor_tensor_scan(T["s4" + k][:], T.rr4[:], T["t2" + k][:], 0.0, OP.add, OP.max))
+        e = under("wb", "mask16", 2)
+        need("v", [d])
+
+        def offsets(i, block, blocks):
+            for b in blocks:
+                off[i] = done("v", V.tensor_scalar(T.off4[32 * b:32 * b + 32, 24 * i:24 * i + 24], T["s4" + k][32 * block:32 * block + 32, 3:CK:4], 4.0, pcol(P3, 32 * b, 32 * b + 32), OP.mult, OP.add))
+
+        def upper(lo, hi):
+            need("v", [off[hi - 1]])
+            d = done("v", V.tensor_copy(T.off4[64:128, 24 * lo:24 * hi], T.off4[0:64, 24 * lo:24 * hi]))
+            for i in range(lo, hi):
+                off[i] = d
+
+        if k == "1":
+            offsets(0, 0, range(4))
+            offsets(1, 1, (0, 1))
+            offsets(2, 2, (0, 1))
+            offsets(3, 3, (0, 1))
+        else:
+            offsets(4, 0, (0, 1))
+            offsets(5, 2, (0, 1))
+        need("v", [e])
+        v_t3[k] = done("v", V.transpose(T["t3" + k][:], T["wb" + k][:]))
+        if k == "1":
+            upper(1, 4)
+        else:
+            upper(4, 6)
+
+    def singles(k):
+        need("v", [v_t3[k]])
+        v_s16[k] = done("v", V.tensor_tensor_scan(T["s16" + k][:], T.rr16[:], T["t3" + k][:], 0.0, OP.add, OP.max))
+
+    def gather(q, e):
+        i = idx[e]
+        out = T.xt[:, 4 * pos[e]:4 * pos[e] + 4 * CK]
+        win = T.xsb[:, 0:4 * NT].indirect(T.off4[:, 24 * i:24 * i + 24])
+        need(q, [off[i], LDX, LDX2])
         return done(q, A.activation(out, win, AF.Copy) if q == "a" else V.tensor_copy(out, win))
 
     def pack(lo, hi, deps, src, qc, qs):
@@ -270,31 +369,69 @@ def rank_program(g, core, T, topo):
 
     DF, DN, RF, RN = ("df", arrivals(True)), ("dn", arrivals(False)), ("rf", arrivals(True)), ("rn", arrivals(False))
 
-    for e in far:
-        offsets(e, "abc")
+    def qweight(i):
+        need("v", [LDW])
+        return done("v", V.quantize_mx(T.qw[:, 128 * i:128 * i + 128], T.pw[:, 128 * i:128 * i + 128], T.w1s[:, 512 * i:512 * i + 512]))
+
+    def qunpack(i):
+        need("v", [c_et[i]])
+        return done("v", V.quantize_mx(T.qe[:, 128 * i:128 * i + 128], T.pe[:, 128 * i:128 * i + 128], T.et[:, 512 * i:512 * i + 512]))
+
+    def filler(steps):
+        steps = list(steps)
+
+        def fill(n=1):
+            for _ in range(min(n, len(steps))):
+                steps.pop(0)()
+        return fill
+
+    R1, R2 = ROUNDS
+    s1, s2 = R1["W"] * R1["NS"], R2["W"] * R2["NS"]
+    d1, d2 = own_mask(R1, 0, s1), own_mask(R1, s1, NT)
+    own_scan(R1, 0, s1, d1)
+    own_scan(R1, s1, NT, d2)
+    scalar_ranks(R1)
+    rr("2")
+    need("a", [c_k4])
+    c_r4 = done("a", A.activation(T.reset4[:], T.k4[:], AF.Sign))
+    c_cl = done("a", A.activation(T.cl[:, NP:NP + NT], T.k1[:], AF.Copy, scale=0.0))
+    md2 = []
+    fill = filler([lambda lo=lo: md2.append(own_mask(R2, lo, lo + 96)) for lo in range(0, NT, 96)])
+    v_win = vector_ranks(R1, fill)
+    lists(R1, v_win, fill)
     for e in far[:2]:
-        gather("a", e)
-    a_gf = gather("a", far[2], 12, 24)
-    v_gf = gather("v", far[2], 0, 12)
-    offsets(near[0], "a")
+        a_gf = gather("a", e)
+    fill(4)
+    v_gf = gather("v", far[2])
     v_qfar = pack(FAR0, NEAR0, [a_gf, v_gf], "xt", "ct", "cs")
     send(True, v_qfar, "ct", "cs", "rxf", "rxfs", "df")
-    spread(me)
-    offsets(near[1], "a")
-    offsets(near[0], "b")
-    offsets(near[1], "b")
-    offsets(near[0], "c")
-    offsets(near[1], "c")
+    c_et += [one_tile(2), one_tile(3)]
+
+    own_scan(R2, 0, s2, md2[-1])
+    own_scan(R2, s2, NT, md2[-1])
+    singles("1")
+    scalar_ranks(R2)
     a_gn = gather("a", near[0])
+
+    def spread(i):
+        k, block = ("1", i) if i < 4 else ("2", 2 * (i - 4))
+        need("a", [v_s16[k]])
+        for b in (0, 1):
+            d = done("a", A.activation(T.offf[32 * b:32 * b + 32, 6 * i:6 * i + 6], T["s16" + k][32 * block:32 * block + 32, 15:CK:16], AF.Copy))
+        return d
+
+    for i in range(4):
+        spread(i)
+    v_qw = []
+    fill = filler([lambda i=i: v_qw.append(qweight(i)) for i in range(4)])
+    fill()
+    v_win = vector_ranks(R2, fill)
+    lists(R2, v_win, fill)
     v_gn = gather("v", near[1])
-    offsets(me, "a")
+    fill(4)
+    singles("2")
     v_qnear = pack(NEAR0, OWN0, [a_gn, v_gn], "xt", "ct", "cs")
     send(False, v_qnear, "ct", "cs", "rxn", "rxns", "dn")
-    offsets(me, "bc")
-    need("a", [c_m16, bc[me]])
-    for m in range(16):
-        a_s16 = done("a", A.activation(T.s16[:, m:576:16], T.bl[:, m:576:16], AF.Copy, scale=T.mcol16[:, m:m + 1]))
-    a_go = gather("a", me)
 
     def products(stat, plane, codes, planes, lo, hi, bank, deps):
         need("t", deps)
@@ -305,13 +442,12 @@ def rank_program(g, core, T, topo):
             r.append(done("t", TE.matmul_mx(T.pp[:, o:o + hi - lo], T[stat][:, c], T[plane][:, c], T[codes][:, lo:hi], T[planes][:, lo:hi], True, True)))
         return r
 
-    def relu(q, lo, hi, bank, i, dep):
-        need(q, [dep])
-        o = 512 * (bank + i)
-        out, src = T.rt[:, 4 * lo + i:4 * hi:4], T.pp[:, o:o + hi - lo]
-        if q == "v":
-            return done("v", V.tensor_scalar(out, src, 0.0, 0.05, OP.max, OP.mult))
-        return done("a", A.activation(out, src, AF.Relu, scale=0.05))
+    def relus(lo, hi, bank, deps):
+        for i in range(4):
+            need("a", [deps[i]])
+            o = 512 * (bank + i)
+            d = done("a", A.activation(T.rt[:, 4 * lo + i:4 * hi:4], T.pp[:, o:o + hi - lo], AF.Relu, scale=0.05))
+        return d
 
     def slot(e):
         return 4 * (1 + CK * e)
@@ -319,8 +455,7 @@ def rank_program(g, core, T, topo):
     def unpack(q, e0, n, bank, col, b, dep):
         need(q, [dep])
         o = 512 * (bank + b) + col
-        t = T.aa if e0 == 0 and n == CK else T.dd
-        out, src = t[:, slot(e0) + b:slot(e0) + 4 * n:4], T.pp[:, o:o + n]
+        out, src = T.aa[:, slot(e0) + b:slot(e0) + 4 * n:4], T.pp[:, o:o + n]
         return done(q, V.tensor_copy(out, src) if q == "v" else A.activation(out, src, AF.Copy))
 
     table = T.cl[:, NP:NP + NT]
@@ -328,101 +463,83 @@ def rank_program(g, core, T, topo):
 
     def tab(k):
         e = (k + 1) // 2
-        o16 = T.off16[:, 6 * e:6 * e + 6]
-        need("v", [tk["last"]])
+        o16 = T.off16[:, 6 * idx[e]:6 * idx[e] + 6]
         if k % 2:
-            tk["last"] = done("v", V.tensor_copy(T.cl[:, CK * (e - 1):CK * e], table.indirect(o16)))
+            need("a", [tk["last"], v_o16])
+            tk["last"] = done("a", A.activation(T.cl[:, CK * (e - 1):CK * e], table.indirect(o16), AF.Copy))
             if e == N - 1:
                 mask(0, NP)
         else:
+            need("v", [tk["last"]])
             tk["last"] = done("v", V.tensor_copy(table.indirect(o16), T.slots[:, CK * e:CK * e + CK]))
 
     def mask(lo, hi):
-        need("a", [tk["last"], c_mcol])
+        need("a", [tk["last"], c_lists])
         for m in range(4):
             tk[lo] = done("a", A.activation(T.cm[:, lo + m:hi:4], T.cl[:, lo + m:hi:4], AF.Copy, scale=T.mcol[:, m:m + 1]))
 
     def wrap(lo, hi):
         need("v", [tk[lo], c_r4])
-        d = done("v", V.tensor_tensor_scan(T.cq[:, lo:hi], T.reset4[:, lo:hi], T.cm[:, lo:hi], 0.0, OP.mult, OP.add))
+        d = done("v", V.tensor_tensor_scan(T.cq[:, lo:hi], T.reset4[:, 0:hi - lo], T.cm[:, lo:hi], 0.0, OP.mult, OP.add))
         need("v", [d])
-        return done("v", V.tensor_scalar(T.offc[:, lo // 4:hi // 4], T.cq[:, lo + 3:hi:4], T.p3[:, 0:1], None, OP.add))
+        return done("v", V.tensor_scalar(T.offc[:, lo // 4:hi // 4], T.cq[:, lo + 3:hi:4], pcol(P3), None, OP.add))
 
-    def qweight(i):
-        need("v", [LDW])
-        return done("v", V.quantize_mx(T.qw[:, 128 * i:128 * i + 128], T.pw[:, 128 * i:128 * i + 128], T.w1s[:, 512 * i:512 * i + 512]))
+    p_far = products("qw", "pw", "rxf", "rxfs", 0, 288, 4, [DF, v_qw[-1]])
+    a_far = relus(FAR0, NEAR0, 4, p_far)
+    spread(4)
+    d = spread(5)
+    need("a", [d])
+    a_offf = done("a", A.activation(T.offf[64:128, :], T.offf[0:64, :], AF.Copy))
+    a_go = gather("a", me)
+    v_rfar = pack(FAR0, NEAR0, [a_far], "rt", "rc", "rs")
+    send(True, v_rfar, "rc", "rs", "bkf", "bkfs", "rf")
 
-    def qunpack(i):
-        need("v", [c_et])
-        return done("v", V.quantize_mx(T.qe[:, 128 * i:128 * i + 128], T.pe[:, 128 * i:128 * i + 128], T.et[:, 512 * i:512 * i + 512]))
-
-    qweight(0)
-    qweight(1)
-    need("v", [a_s16])
-    d = done("v", V.tensor_tensor_scan(T.s16b[:], T.reset16[:], T.s16[:], 0.0, OP.mult, OP.add))
-    qweight(2)
-    need("v", [d])
-    v_o16 = done("v", V.tensor_copy(T.off16[:], T.s16b[:, 15:576:16]))
-    v_qw = qweight(3)
+    need("v", [a_offf])
+    v_o16 = done("v", V.tensor_copy(T.off16[:], T.offf[:]))
+    qunpack(0)
     need("v", [v_o16, c_cl, c_slots])
     tab(0)
     v_qown = pack(OWN0, ALLC, [a_go, c_xpad], "xt", "ct", "cs")
     tab(1)
-    qunpack(0)
+    p_own = products("qw", "pw", "ct", "cs", OWN0, ALLC, 0, [v_qown, v_eq["2"], a_acc["2"], v_win])
+    a_own = relus(OWN0, ALLC, 0, p_own)
     tab(2)
-    qunpack(1)
     tab(3)
-    p_own = products("qw", "pw", "ct", "cs", OWN0, ALLC, 0, [v_qw, v_qown, v_eq, a_acc])
-    r1 = [relu("v", OWN0, ALLC, 0, i, p_own[i]) for i in (0, 1)]
-    r2 = [relu("a", OWN0, ALLC, 0, i, p_own[i]) for i in (2, 3)]
+    qunpack(1)
+    v_rown = pack(OWN0, ALLC, [a_own], "rt", "rc", "rs")
     tab(4)
-    v_rown = pack(OWN0, ALLC, [r1[-1], r2[-1]], "rt", "rc", "rs")
-
-    p_far = products("qw", "pw", "rxf", "rxfs", 0, 288, 4, [DF])
-    f1 = [relu("v", FAR0, NEAR0, 4, i, p_far[i]) for i in (0, 2)]
-    f2 = [relu("a", FAR0, NEAR0, 4, i, p_far[i]) for i in (1, 3)]
-    v_rfar = pack(FAR0, NEAR0, [f1[-1], f2[-1]], "rt", "rc", "rs")
-    send(True, v_rfar, "rc", "rs", "bkf", "bkfs", "rf")
+    p_near = products("qw", "pw", "rxn", "rxns", 0, 192, 4, [DN, a_far])
+    a_near = relus(NEAR0, OWN0, 4, p_near)
     qunpack(2)
     v_qe = qunpack(3)
-
-    p_near = products("qw", "pw", "rxn", "rxns", 0, 192, 0, [DN, r1[-1], r2[-1]])
-    e_near = [relu("va"[i % 2], NEAR0, OWN0, 0, i, p_near[i]) for i in range(4)][2:]
-    v_rnear = pack(NEAR0, OWN0, e_near, "rt", "rc", "rs")
+    v_rnear = pack(NEAR0, OWN0, [a_near], "rt", "rc", "rs")
     send(False, v_rnear, "rc", "rs", "bkn", "bkns", "rn")
-
-    u_own = products("qe", "pe", "rc", "rs", OWN0, ALLC, 4, [v_rown, v_qe, f1[-1], f2[-1]])
-    d_own = [unpack("a", me, CK, 4, 0, b, u_own[b]) for b in range(4)]
-
     for k in range(5, 2 * N - 1):
         tab(k)
-    v_prev = wrap(0, NP)
     mask(NP, NP + NT)
+
+    u_own = products("qe", "pe", "rc", "rs", OWN0, ALLC, 0, [v_rown, v_qe, a_own])
+    d_own = [unpack("a", me, CK, 0, 0, b, u_own[b]) for b in range(4)]
+    v_prev = wrap(0, NP)
     v_last = wrap(NP, NP + NT)
 
-    u_near = products("qe", "pe", "bkn", "bkns", 0, 192, 0, [RN] + e_near)
-    d_near = [unpack("a", near[i], CK, 0, CK * i, b, u_near[b]) for b in range(4) for i in range(2)]
-    u_far = products("qe", "pe", "bkf", "bkfs", 0, 288, 4, [RF, d_own[-1]])
+    u_near = products("qe", "pe", "bkn", "bkns", 0, 192, 4, [RN, a_near])
+    d_near = [unpack("a", near[i], CK, 4, CK * i, b, u_near[b]) for b in range(4) for i in range(2)]
+    u_far = products("qe", "pe", "bkf", "bkfs", 0, 288, 0, [RF, d_own[-1]])
 
     def chain(e, deps):
         need("v", deps + [v_prev, c_aa])
         o = 24 * (e - 1)
         s = slice(slot(e), slot(e) + 4 * CK)
-        return done("v", V.tensor_tensor(T.aa[:, s], T.aa[:, 0:slot(e)].indirect(T.offc[:, o:o + 24]), T.dd[:, s], OP.add))
-
-    def far_unpack(q, b):
-        if far[0] == 0:
-            unpack(q, 0, CK, 4, 0, b, u_far[b])
-            return unpack(q, 1, 2 * CK, 4, CK, b, u_far[b])
-        return unpack(q, far[0], 3 * CK, 4, 0, b, u_far[b])
+        return done("v", V.tensor_tensor(T.aa[:, s], T.aa[:, 0:slot(e)].indirect(T.offc[:, o:o + 24]), T.aa[:, s], OP.add))
 
     dlast = [d_own[-1], d_near[-1]]
     step = None
     if far[0] != 0:
         for e in (1, 2):
             step = chain(e, dlast + [step])
-    d1 = [far_unpack("v", b) for b in (0, 1)][-1]
-    d2 = [far_unpack("a", b) for b in (2, 3)][-1]
+    d1 = [unpack("v", far[0], 3 * CK, 0, 0, b, u_far[b]) for b in (0, 1)][-1]
+    d2 = [unpack("a", far[0], 3 * CK, 0, 0, b, u_far[b]) for b in (2, 3)][-1]
     for e in range(1 if far[0] == 0 else 3, N):
         step = chain(e, dlast + [d1, d2, step])
 

from concourse.bass import DstId, RemoteDMATransfer
from concourse.mybir import dt, AluOpType, ActivationFunctionType

OP = AluOpType
AF = ActivationFunctionType
NT, CK, N = 384, 96, 6
BIG = 1e29
F8, U8, F32, BF, U16, I32 = "float8_e4m3fn_x4", "uint8", "float32", "bfloat16", "uint16", "int32"

FAR0, NEAR0, OWN0, ALLC = 0, 3 * CK, 5 * CK, 5 * CK + 128
HALF = NT // 2
NP = CK * (N - 1)
ROUNDS = ({"k": "1", "W": 32, "NS": 5, "bank": 0}, {"k": "2", "W": 64, "NS": 3, "bank": 2})

SHAPES = {
    BF: {"xsb": 4 * NT, "wgs": 32, "wga1": 512, "wga2": 512, "w1s": 2048, "ones": 512, "et": 2048, "reset1": NT, "reset2": NT,
         "reset4": NP, "xt": 4 * ALLC, "rt": 4 * ALLC},
    F8: {"qx": NT, "qg1": 128, "qg2": 128, "qw": 512, "qe": 512, "ct": ALLC, "rxn": 192, "rxf": 288, "rc": ALLC, "bkn": 192, "bkf": 288},
    U8: {"px": NT, "pg1": 128, "pg2": 128, "pw": 512, "pe": 512, "cs": ALLC, "rxns": 192, "rxfs": 288, "rs": ALLC, "bkns": 192, "bkfs": 288},
    I32: {"pi": 2, "pci": 8},
    U16: {"offw": 64, "off4": 144, "off16": 36, "offc": 216},
    F32: {"pc": 8, "offwf": 64, "k1": NT, "k2": NT, "im4": 32, "im16": 32, "k4s": CK, "k16s": CK, "k4": NP, "cut1": 12, "cut2": 6,
          "slots": 576, "mask4": 32, "mask16": 32, "rr4": CK, "rr16": CK, "mcol": 4, "v2": 6, "offf": 36,
          "cl": NP + NT, "cm": NP + NT, "cq": NP + NT, "aa": 8 + 4 * 576, "yy": 4 * NT},
}
for R in ROUNDS:
    k, n, ns = R["k"], NT // R["W"], R["NS"]
    R["n"] = n
    SHAPES[BF].update({"cmp" + k: n * NT, "sums" + k: (n - ns) * HALF, "eqw" + k: NT, "corr" + k: NT})
    SHAPES[U16].update({"offr" + k: n})
    SHAPES[F32].update({"m3" + k: NT, "rr" + k: NT, "md" + k: NT, "sc" + k: NT, "acc" + k: ns, "accb" + k: ns, "accc" + k: ns, "rk" + k: ns, "rkb" + k: ns,
                        "first" + k: n, "tok" + k: 16 * n, "tokf" + k: 16 * n, "win" + k: NT, "t1" + k: CK, "wa" + k: CK, "t2" + k: CK, "s4" + k: CK,
                        "wb" + k: CK, "t3" + k: CK, "s16" + k: CK})
SCRATCH = {name: ("sbuf", [128, n], kind) for kind in SHAPES for name, n in SHAPES[kind].items()}
SCRATCH["pp"] = ("psum", [128, 4096], F32)
SEMAPHORES = ["sv", "sa", "sten", "sp", "ldx", "ldx2", "ldg", "ldw", "sty", "sty2", "loc", "dn", "df", "rn", "rf"]


def rank_program(g, core, T, topo):
    me = T.rank_of(core)
    if me is None:
        return
    cores = list(T.cores)

    def far_of(r):
        return [k for k in range(N) if topo.chip(cores[k]) != topo.chip(cores[r])]

    def near_of(r):
        return [k for k in range(N) if k != r and topo.chip(cores[k]) == topo.chip(cores[r])]

    far, near = far_of(me), near_of(me)
    order = far + near + [me]
    idx = {e: i for i, e in enumerate(order)}
    pos = {e: CK * idx[e] for e in order}

    Q = {"v": (g.vector, "sv"), "a": (g.scalar, "sa"), "t": (g.tensor, "sten"), "p": (g, "sp"), "s": (g.sync, None)}
    count = {"sv": 0, "sa": 0, "sten": 0, "sp": 0}
    seen = {}

    def need(q, deps):
        for d in deps:
            if d is not None and seen.get((q, d[0]), 0) < d[1]:
                Q[q][0].wait_ge(T.sem[d[0]], d[1])
                seen[(q, d[0])] = d[1]

    def done(q, ins):
        s = Q[q][1]
        ins.then_inc(T.sem[s], 1)
        count[s] += 1
        if q == "p":
            need("p", [(s, count[s])])
        return (s, count[s])

    V, A, TE = g.vector, g.scalar, g.tensor

    g.sync.dma_start(T.xsb[:, 0:4 * HALF], T.x[:, 0:4 * HALF]).then_inc(T.sem["ldx"], 16)
    g.scalar.dma_start(T.wgs[:], T.wg[:, 0:32]).then_inc(T.sem["ldg"], 16)
    g.sync.dma_start(T.xsb[:, 4 * HALF:4 * NT], T.x[:, 4 * HALF:4 * NT]).then_inc(T.sem["ldx2"], 16)
    g.sync.dma_start(T.w1s[:], T.w1[:]).then_inc(T.sem["ldw"], 16)
    LDX, LDX2, LDG, LDW = ("ldx", 16), ("ldx2", 16), ("ldg", 16), ("ldw", 16)

    def iota(name, pattern, base=0, cm=0):
        if name == "pi":
            return done("p", g.iota(T.pi[:], pattern, base, cm))
        return done("p", g.iota(T[name][:], pattern, base, cm, allow_small_or_imprecise_dtypes=True))

    c_pi = iota("pi", [[0, 2]], 0, 1)
    c_k = {"1": iota("k1", [[0, 12], [1, 32]])}
    c_im4 = iota("im4", [[0, 2], [1, 4], [0, 4]])
    c_im16 = iota("im16", [[0, 2], [1, 16]])
    c_k4s = iota("k4s", [[0, 24], [1, 4]])
    c_k16s = iota("k16s", [[0, 6], [1, 16]])
    c_cut = {"1": iota("cut1", [[32, 12]], 32)}
    c_k["2"] = iota("k2", [[0, 6], [1, 64]])
    c_tokf = {"1": iota("tokf1", [[32, 12], [1, 16]]), "2": iota("tokf2", [[64, 6], [1, 16]])}
    c_cut["2"] = iota("cut2", [[64, 6]], 64)
    c_slots = iota("slots", [[1, 576]], 1)
    c_k4 = iota("k4", [[0, NP // 4], [1, 4]])

    for i in range(4):
        done("v", V.memset(T.offwf[:, 8 * i:8 * i + 8], float(4 * order[i])))
    for i in (4, 5):
        c_offwf = done("v", V.memset(T.offwf[:, 16 * i - 32:16 * i - 16], float(4 * order[i])))
    c_ones = done("v", V.memset(T.ones[:], 1.0))
    P3, P15, W31, W63, H16, H48, PM = range(7)
    need("v", [c_pi])
    for k, m in enumerate((3, 15, 31, 63, 16, 48)):
        done("v", V.tensor_scalar(T.pci[:, k:k + 1], T.pi[:, 0:1], m, None, OP.bitwise_and))
    done("v", V.tensor_scalar(T.pci[:, PM:PM + 1], T.pi[:, 0:1], 15, 2, OP.bitwise_and, OP.logical_shift_right))
    d = done("v", V.tensor_scalar(T.pci[:, 7:8], T.pi[:, 0:1], 0, None, OP.bitwise_and))
    c_win = [done("v", V.memset(T[w][:, 0:CK], 0.0)) for w in ("win1", "win2")][-1]
    need("v", [d])
    c_pc = done("v", V.tensor_copy(T.pc[:], T.pci[:]))
    c_v2 = done("v", V.memset(T.v2[:], 0.0))

    def pcol(k, lo=0, hi=128):
        return T.pc[lo:hi, k:k + 1]

    need("v", [c_offwf, c_pc])
    c_offw = done("v", V.tensor_scalar(T.offw[:], T.offwf[:], pcol(P3), None, OP.add))
    c_m3 = {}

    def m3(k, col):
        need("v", [c_k[k]])
        c_m3[k] = done("v", V.tensor_scalar(T["m3" + k][:], T["k" + k][:], pcol(col), -BIG, OP.not_equal, OP.mult))

    m3("1", W31)
    c_xpad = done("v", V.memset(T.xt[:, 4 * (OWN0 + CK):4 * ALLC], 0.0))
    c_aa = done("v", V.memset(T.aa[:, 0:4], 0.0))

    c_reset, c_rr, c_tok, a_wga = {}, {}, {}, {}

    def reset(k):
        need("a", [c_k[k]])
        c_reset[k] = done("a", A.activation(T["reset" + k][:], T["k" + k][:], AF.Sign))

    def rr(k):
        need("a", [c_reset[k]])
        c_rr[k] = done("a", A.activation(T["rr" + k][:], T["reset" + k][:], AF.Copy, bias=-BIG, scale=BIG))

    def tokens(k, col):
        need("a", [c_tokf[k], c_pc])
        c_tok[k] = done("a", A.activation(T["tok" + k][:], T["tokf" + k][:], AF.Identity, bias=pcol(col)))

    def gates(k, lo):
        need("a", [c_offw, LDG])
        a_wga[k] = done("a", A.activation(T["wga" + k][:], T.wgs[:, 0:32].indirect(T.offw[:, lo:lo + 32]), AF.Copy))

    reset("1")
    gates("1", 0)
    rr("1")
    gates("2", 32)
    tokens("1", H16)
    reset("2")
    tokens("2", H48)

    need("p", [c_ones])

    def one_tile(b):
        return done("p", g.affine_select(T.et[:, 512 * b:512 * b + 512], T.ones[:], [[-1, 512]], OP.is_equal, 0.0, b, 4))

    c_et = [one_tile(0), one_tile(1)]

    need("v", [a_wga["1"]])
    done("v", V.quantize_mx(T.qg1[:], T.pg1[:], T.wga1[:]))
    need("v", [LDX])
    done("v", V.quantize_mx(T.qx[:, 0:HALF], T.px[:, 0:HALF], T.xsb[:, 0:4 * HALF]))
    need("v", [c_im4, c_im16, c_k4s, c_k16s])
    done("v", V.tensor_scalar(T.mask4[:], T.im4[:], pcol(P3), -BIG, OP.not_equal, OP.mult))
    done("v", V.tensor_scalar(T.mask16[:], T.im16[:], pcol(P15), -BIG, OP.not_equal, OP.mult))
    done("v", V.tensor_scalar(T.mcol[:], T.k4s[:, 0:4], pcol(PM), 4.0, OP.is_equal, OP.mult))
    done("v", V.tensor_scalar(T.rr4[:], T.k4s[:], 0.0, -BIG, OP.is_equal, OP.mult))
    c_lists = done("v", V.tensor_scalar(T.rr16[:], T.k16s[:], 0.0, -BIG, OP.is_equal, OP.mult))
    need("v", [LDX2])
    v_qx = done("v", V.quantize_mx(T.qx[:, HALF:NT], T.px[:, HALF:NT], T.xsb[:, 4 * HALF:4 * NT]))
    m3("2", W63)
    need("v", [a_wga["2"]])
    v_qg2 = done("v", V.quantize_mx(T.qg2[:], T.pg2[:], T.wga2[:]))
    t_z = {}
    for R, dep in zip(ROUNDS, (v_qx, v_qg2)):
        k = R["k"]
        need("t", [dep])
        t_z[k] = [done("t", TE.matmul_mx(T.pp[:, 512 * b:512 * b + NT], T["qg" + k][:], T["pg" + k][:], T.qx[:], T.px[:], True, True)) for b in (R["bank"], R["bank"] + 1)]

    def z(R, other, lo=0, hi=NT):
        o = 512 * (R["bank"] + other)
        return T.pp[:, o + lo:o + hi]

    v_sc = {}

    def own_mask(R, lo, hi):
        k = R["k"]
        need("v", [t_z[k][0], c_m3[k]])
        return done("v", V.tensor_tensor(T["md" + k][:, lo:hi], z(R, 0, lo, hi), T["m3" + k][:, lo:hi], OP.add))

    def own_scan(R, lo, hi, dep):
        k = R["k"]
        need("v", [dep, c_rr[k]])
        v_sc[k + str(lo)] = done("v", V.tensor_tensor_scan(T["sc" + k][:, lo:hi], T["rr" + k][:, lo:hi], T["md" + k][:, lo:hi], 0.0, OP.add, OP.max))

    a_acc = {}

    def scalar_ranks(R):
        k, W, ns = R["k"], R["W"], R["NS"]
        need("a", [t_z[k][1], v_sc[k + "0"]])
        cmp, signs = T["cmp" + k], []
        for q in range(ns + 1):
            if q < ns:
                signs.append(done("a", A.activation(cmp[:, NT * q:NT * q + NT], z(R, 1), AF.Sign, bias=T["sc" + k][:, W * q + W - 1:W * q + W], scale=-1.0)))
            if q:
                j, c = q - 1, NT * (q - 1)
                lower, higher = cmp[:, c:c + W * q], cmp[:, c + W * q:c + NT]
                need("a", [signs[j]])
                done("a", A.activation(lower, lower, AF.Relu, accum_out=T["acc" + k][:, j:j + 1]))
                a_acc[k] = done("a", A.activation(higher, higher, AF.Relu, scale=-1.0, accum_out=T["accb" + k][:, j:j + 1]))

    v_eq = {}

    def vector_ranks(R, fill):
        k, W, ns, n = R["k"], R["W"], R["NS"], R["n"]
        cmp, sc, corr, first, offr = T["cmp" + k], T["sc" + k], T["corr" + k], T["first" + k], T["offr" + k]
        s0 = W * ns

        def total(q, deps):
            o, c = HALF * (q - ns), NT * q
            need("v", deps)
            return done("v", V.tensor_tensor_scan(T["sums" + k][:, o:o + HALF], cmp[:, c:c + HALF], cmp[:, c + HALF:c + NT], first[:, q:q + 1], OP.add, OP.add))

        need("v", [v_sc[k + str(s0)]])
        v_eq[k] = done("v", V.tensor_tensor(T["eqw" + k][:], z(R, 0), sc[:], OP.is_equal))
        late = []
        for q in range(ns, n):
            s = sc[:, W * q + W - 1:W * q + W]
            cut, c = W * q + W, NT * q
            d = done("v", V.tensor_scalar(cmp[:, c:c + cut], z(R, 0, 0, cut), s, None, OP.is_ge))
            if cut < NT:
                d = done("v", V.tensor_scalar(cmp[:, c + cut:c + NT], z(R, 0, cut, NT), s, None, OP.is_gt))
            late.append((q, d))
            if q == ns:
                need("v", [v_eq[k], c_reset[k]])
                v_corr = done("v", V.tensor_tensor_scan(corr[:], T["reset" + k][:], T["eqw" + k][:], 0.0, OP.mult, OP.add))
            elif q == ns + 1:
                need("v", [v_corr, c_cut[k]])
                v_first = done("v", V.tensor_scalar(first[:], corr[:, W - 1:NT:W], -1.0, -float(HALF), OP.mult, OP.add))
                v_k = done("v", V.tensor_tensor(T["rkb" + k][:], T["cut" + k][:, 0:ns], corr[:, W - 1:s0:W], OP.subtract))
            else:
                j, d = late.pop(0)
                total(j, [d, v_first])
        j, d = late.pop(0)
        total(j, [d, v_first])
        need("v", [a_acc[k], v_k])
        d0 = done("v", V.tensor_tensor(T["accc" + k][:], T["accb" + k][:], T["acc" + k][:], OP.subtract))
        j, d = late.pop(0)
        v_sum = total(j, [d])
        need("v", [d0])
        d0 = done("v", V.tensor_tensor(T["rk" + k][:], T["accc" + k][:], T["rkb" + k][:], OP.add))
        need("v", [v_sum])
        done("v", V.tensor_scalar(offr[:, ns:n], T["sums" + k][:, HALF - 1:HALF * (n - ns):HALF], float(HALF), None, OP.add))
        need("v", [d0])
        v_offr = done("v", V.tensor_copy(offr[:, 0:ns], T["rk" + k][:]))
        fill()
        need("v", [v_offr, c_tok[k], c_win])
        return done("v", V.tensor_copy(T["win" + k][:, 0:NT].indirect(offr[:, 0:n]), T["tok" + k][:]))

    v_t3, v_s16, off = {}, {}, {}

    def lists(R, v_win, fill):
        k = R["k"]
        t1 = T["t1" + k]
        fill()
        need("v", [v_win, c_lists])
        d = done("v", V.transpose(t1[:], T["win" + k][:, 0:CK]))
        fill()
        need("v", [d])
        if k == "1":
            pair = [(t1[:, 32 * u:32 * u + 1], t1[:, 32 * u + 16:32 * u + 17]) for u in range(3)]
        else:
            for b in (0, 64):
                d = done("v", V.tensor_tensor(T.v2[b:b + 32, :], t1[b:b + 32, 0:CK:16], t1[b + 32:b + 64, 0:CK:16], OP.add))
            pair = [(T.v2[:, 2 * u:2 * u + 1], T.v2[:, 2 * u + 1:2 * u + 2]) for u in range(3)]
            fill()
            need("v", [d, c_v2])

        def under(w, mask, u):
            return done("v", V.tensor_scalar(T[w + k][:, 32 * u:32 * u + 32], T[mask][:], pair[u][0], pair[u][1], OP.add, OP.add))

        d = [under("wa", "mask4", u) for u in range(3)][-1]
        under("wb", "mask16", 0)
        need("v", [d])
        d = done("v", V.transpose(T["t2" + k][:], T["wa" + k][:]))
        under("wb", "mask16", 1)
        need("v", [d])
        d = done("v", V.tensor_tensor_scan(T["s4" + k][:], T.rr4[:], T["t2" + k][:], 0.0, OP.add, OP.max))
        e = under("wb", "mask16", 2)
        need("v", [d])

        def offsets(i, block, blocks):
            for b in blocks:
                off[i] = done("v", V.tensor_scalar(T.off4[32 * b:32 * b + 32, 24 * i:24 * i + 24], T["s4" + k][32 * block:32 * block + 32, 3:CK:4], 4.0, pcol(P3, 32 * b, 32 * b + 32), OP.mult, OP.add))

        def upper(lo, hi):
            need("v", [off[hi - 1]])
            d = done("v", V.tensor_copy(T.off4[64:128, 24 * lo:24 * hi], T.off4[0:64, 24 * lo:24 * hi]))
            for i in range(lo, hi):
                off[i] = d

        if k == "1":
            offsets(0, 0, range(4))
            offsets(1, 1, (0, 1))
            offsets(2, 2, (0, 1))
            offsets(3, 3, (0, 1))
        else:
            offsets(4, 0, (0, 1))
            offsets(5, 2, (0, 1))
        need("v", [e])
        v_t3[k] = done("v", V.transpose(T["t3" + k][:], T["wb" + k][:]))
        if k == "1":
            upper(1, 4)
        else:
            upper(4, 6)

    def singles(k):
        need("v", [v_t3[k]])
        v_s16[k] = done("v", V.tensor_tensor_scan(T["s16" + k][:], T.rr16[:], T["t3" + k][:], 0.0, OP.add, OP.max))

    def gather(q, e):
        i = idx[e]
        out = T.xt[:, 4 * pos[e]:4 * pos[e] + 4 * CK]
        win = T.xsb[:, 0:4 * NT].indirect(T.off4[:, 24 * i:24 * i + 24])
        need(q, [off[i], LDX, LDX2])
        return done(q, A.activation(out, win, AF.Copy) if q == "a" else V.tensor_copy(out, win))

    def pack(lo, hi, deps, src, qc, qs):
        need("v", deps)
        return done("v", V.quantize_mx(T[qc][:, lo:hi], T[qs][:, lo:hi], T[src][:, 4 * lo:4 * hi]))

    local = [0]

    def lanes(isfar, bits, i):
        if not isfar:
            return (8 + 4 * i, 12 + 4 * i)
        return (2 * i, 2 * i + 2) if bits else ((6, 7), (7, 8), (0, 4))[i]

    def arrivals(isfar):
        n = 0
        for r in (far if isfar else near):
            i = (far_of(r) if isfar else near_of(r)).index(me)
            for bits in (True, False):
                lo, hi = lanes(isfar, bits, i)
                n += hi - lo
        return n

    def send(isfar, dep, codes, planes, dcodes, dplanes, rsem):
        need("p", [dep])
        for bits, sname, dname in ((True, codes, dcodes), (False, planes, dplanes)):
            tr = []
            for i, r in enumerate(far if isfar else near):
                lo, hi = lanes(isfar, bits, i)
                es = topo.engines(core, cores[r])[lo:hi]
                there = (far_of(r) if isfar else near_of(r)).index(me) * CK
                src = T[sname][:, pos[r]:pos[r] + CK]
                dst = T[dname][:, there:there + CK]
                if bits:
                    src, dst = src.bitcast(dt.uint8), dst.bitcast(dt.uint8)
                ad = topo.addr(cores[r])
                tr.append(RemoteDMATransfer(dst_ids=[DstId(rid=ad[0], pnc=ad[1])], dma_engine_mask=sum(1 << k for k in es), remote_sem=T.sem[rsem], src=src, dst=dst))
                local[0] += len(es)
            g.remote_dma_fused(tr, local_sem=T.sem["loc"])

    DF, DN, RF, RN = ("df", arrivals(True)), ("dn", arrivals(False)), ("rf", arrivals(True)), ("rn", arrivals(False))

    def qweight(i):
        need("v", [LDW])
        return done("v", V.quantize_mx(T.qw[:, 128 * i:128 * i + 128], T.pw[:, 128 * i:128 * i + 128], T.w1s[:, 512 * i:512 * i + 512]))

    def qunpack(i):
        need("v", [c_et[i]])
        return done("v", V.quantize_mx(T.qe[:, 128 * i:128 * i + 128], T.pe[:, 128 * i:128 * i + 128], T.et[:, 512 * i:512 * i + 512]))

    def filler(steps):
        steps = list(steps)

        def fill(n=1):
            for _ in range(min(n, len(steps))):
                steps.pop(0)()
        return fill

    R1, R2 = ROUNDS
    s1, s2 = R1["W"] * R1["NS"], R2["W"] * R2["NS"]
    d1, d2 = own_mask(R1, 0, s1), own_mask(R1, s1, NT)
    own_scan(R1, 0, s1, d1)
    own_scan(R1, s1, NT, d2)
    scalar_ranks(R1)
    rr("2")
    need("a", [c_k4])
    c_r4 = done("a", A.activation(T.reset4[:], T.k4[:], AF.Sign))
    c_cl = done("a", A.activation(T.cl[:, NP:NP + NT], T.k1[:], AF.Copy, scale=0.0))
    md2 = []
    fill = filler([lambda lo=lo: md2.append(own_mask(R2, lo, lo + 96)) for lo in range(0, NT, 96)])
    v_win = vector_ranks(R1, fill)
    lists(R1, v_win, fill)
    for e in far[:2]:
        a_gf = gather("a", e)
    fill(4)
    v_gf = gather("v", far[2])
    v_qfar = pack(FAR0, NEAR0, [a_gf, v_gf], "xt", "ct", "cs")
    send(True, v_qfar, "ct", "cs", "rxf", "rxfs", "df")
    c_et += [one_tile(2), one_tile(3)]

    own_scan(R2, 0, s2, md2[-1])
    own_scan(R2, s2, NT, md2[-1])
    singles("1")
    scalar_ranks(R2)
    a_gn = gather("a", near[0])

    def spread(i):
        k, block = ("1", i) if i < 4 else ("2", 2 * (i - 4))
        need("a", [v_s16[k]])
        for b in (0, 1):
            d = done("a", A.activation(T.offf[32 * b:32 * b + 32, 6 * i:6 * i + 6], T["s16" + k][32 * block:32 * block + 32, 15:CK:16], AF.Copy))
        return d

    for i in range(4):
        spread(i)
    v_qw = []
    fill = filler([lambda i=i: v_qw.append(qweight(i)) for i in range(4)])
    fill()
    v_win = vector_ranks(R2, fill)
    lists(R2, v_win, fill)
    v_gn = gather("v", near[1])
    fill(4)
    singles("2")
    v_qnear = pack(NEAR0, OWN0, [a_gn, v_gn], "xt", "ct", "cs")
    send(False, v_qnear, "ct", "cs", "rxn", "rxns", "dn")

    def products(stat, plane, codes, planes, lo, hi, bank, deps):
        need("t", deps)
        r = []
        for i in range(4):
            c = slice(128 * i, 128 * i + 128)
            o = 512 * (bank + i)
            r.append(done("t", TE.matmul_mx(T.pp[:, o:o + hi - lo], T[stat][:, c], T[plane][:, c], T[codes][:, lo:hi], T[planes][:, lo:hi], True, True)))
        return r

    def relus(lo, hi, bank, deps):
        for i in range(4):
            need("a", [deps[i]])
            o = 512 * (bank + i)
            d = done("a", A.activation(T.rt[:, 4 * lo + i:4 * hi:4], T.pp[:, o:o + hi - lo], AF.Relu, scale=0.05))
        return d

    def slot(e):
        return 4 * (1 + CK * e)

    def unpack(q, e0, n, bank, col, b, dep):
        need(q, [dep])
        o = 512 * (bank + b) + col
        out, src = T.aa[:, slot(e0) + b:slot(e0) + 4 * n:4], T.pp[:, o:o + n]
        return done(q, V.tensor_copy(out, src) if q == "v" else A.activation(out, src, AF.Copy))

    table = T.cl[:, NP:NP + NT]
    tk = {"last": None}

    def tab(k):
        e = (k + 1) // 2
        o16 = T.off16[:, 6 * idx[e]:6 * idx[e] + 6]
        if k % 2:
            need("a", [tk["last"], v_o16])
            tk["last"] = done("a", A.activation(T.cl[:, CK * (e - 1):CK * e], table.indirect(o16), AF.Copy))
            if e == N - 1:
                mask(0, NP)
        else:
            need("v", [tk["last"]])
            tk["last"] = done("v", V.tensor_copy(table.indirect(o16), T.slots[:, CK * e:CK * e + CK]))

    def mask(lo, hi):
        need("a", [tk["last"], c_lists])
        for m in range(4):
            tk[lo] = done("a", A.activation(T.cm[:, lo + m:hi:4], T.cl[:, lo + m:hi:4], AF.Copy, scale=T.mcol[:, m:m + 1]))

    def wrap(lo, hi):
        need("v", [tk[lo], c_r4])
        d = done("v", V.tensor_tensor_scan(T.cq[:, lo:hi], T.reset4[:, 0:hi - lo], T.cm[:, lo:hi], 0.0, OP.mult, OP.add))
        need("v", [d])
        return done("v", V.tensor_scalar(T.offc[:, lo // 4:hi // 4], T.cq[:, lo + 3:hi:4], pcol(P3), None, OP.add))

    p_far = products("qw", "pw", "rxf", "rxfs", 0, 288, 4, [DF, v_qw[-1]])
    a_far = relus(FAR0, NEAR0, 4, p_far)
    spread(4)
    d = spread(5)
    need("a", [d])
    a_offf = done("a", A.activation(T.offf[64:128, :], T.offf[0:64, :], AF.Copy))
    a_go = gather("a", me)
    v_rfar = pack(FAR0, NEAR0, [a_far], "rt", "rc", "rs")
    send(True, v_rfar, "rc", "rs", "bkf", "bkfs", "rf")

    need("v", [a_offf])
    v_o16 = done("v", V.tensor_copy(T.off16[:], T.offf[:]))
    qunpack(0)
    need("v", [v_o16, c_cl, c_slots])
    tab(0)
    v_qown = pack(OWN0, ALLC, [a_go, c_xpad], "xt", "ct", "cs")
    tab(1)
    p_own = products("qw", "pw", "ct", "cs", OWN0, ALLC, 0, [v_qown, v_eq["2"], a_acc["2"], v_win])
    a_own = relus(OWN0, ALLC, 0, p_own)
    tab(2)
    tab(3)
    qunpack(1)
    v_rown = pack(OWN0, ALLC, [a_own], "rt", "rc", "rs")
    tab(4)
    p_near = products("qw", "pw", "rxn", "rxns", 0, 192, 4, [DN, a_far])
    a_near = relus(NEAR0, OWN0, 4, p_near)
    qunpack(2)
    v_qe = qunpack(3)
    v_rnear = pack(NEAR0, OWN0, [a_near], "rt", "rc", "rs")
    send(False, v_rnear, "rc", "rs", "bkn", "bkns", "rn")
    for k in range(5, 2 * N - 1):
        tab(k)
    mask(NP, NP + NT)

    u_own = products("qe", "pe", "rc", "rs", OWN0, ALLC, 0, [v_rown, v_qe, a_own])
    d_own = [unpack("a", me, CK, 0, 0, b, u_own[b]) for b in range(4)]
    v_prev = wrap(0, NP)
    v_last = wrap(NP, NP + NT)

    u_near = products("qe", "pe", "bkn", "bkns", 0, 192, 4, [RN, a_near])
    d_near = [unpack("a", near[i], CK, 4, CK * i, b, u_near[b]) for b in range(4) for i in range(2)]
    u_far = products("qe", "pe", "bkf", "bkfs", 0, 288, 0, [RF, d_own[-1]])

    def chain(e, deps):
        need("v", deps + [v_prev, c_aa])
        o = 24 * (e - 1)
        s = slice(slot(e), slot(e) + 4 * CK)
        return done("v", V.tensor_tensor(T.aa[:, s], T.aa[:, 0:slot(e)].indirect(T.offc[:, o:o + 24]), T.aa[:, s], OP.add))

    dlast = [d_own[-1], d_near[-1]]
    step = None
    if far[0] != 0:
        for e in (1, 2):
            step = chain(e, dlast + [step])
    d1 = [unpack("v", far[0], 3 * CK, 0, 0, b, u_far[b]) for b in (0, 1)][-1]
    d2 = [unpack("a", far[0], 3 * CK, 0, 0, b, u_far[b]) for b in (2, 3)][-1]
    for e in range(1 if far[0] == 0 else 3, N):
        step = chain(e, dlast + [d1, d2, step])

    win = T.aa[:, 0:slot(N)]
    for q, quarters in (("v", (0, 1)), ("a", (2, 3))):
        need(q, [step, v_last])
        r = []
        for k in quarters:
            o = NP // 4 + 24 * k
            out, src = T.yy[:, NT * k:NT * k + NT], win.indirect(T.offc[:, o:o + 24])
            r.append(done(q, V.tensor_copy(out, src) if q == "v" else A.activation(out, src, AF.Copy)))
        dq, sem = ("s", "sty") if q == "v" else ("a", "sty2")
        for k, d in zip(quarters, r):
            need(dq, [d])
            Q[dq][0].dma_start(T.y[:, NT * k:NT * k + NT], T.yy[:, NT * k:NT * k + NT]).then_inc(T.sem[sem], 16)

    g.wait_ge(T.sem["loc"], local[0])
    for s in count:
        g.wait_ge(T.sem[s], count[s])
    g.wait_ge(T.sem["sty"], 32)
    g.wait_ge(T.sem["sty2"], 32)
